import numpy as np
import ml_dtypes


def mxq(x, axis, fmt="e4m3"):
    dtype, down = {"e4m3": (ml_dtypes.float8_e4m3fn, 7), "e5m2": (ml_dtypes.float8_e5m2, 14)}[fmt]
    v = np.moveaxis(np.asarray(x, np.float32).astype(ml_dtypes.bfloat16).astype(np.float64), axis, -1)
    blocks = v.reshape(v.shape[:-1] + (-1, 32))
    amax = np.abs(blocks).max(-1, keepdims=True)
    byte = np.maximum(np.where(amax > 0, np.frexp(amax)[1] - 1 + 127, 0) - down, 1)
    scale = np.exp2(byte - 127.0)
    codes = (blocks / scale).astype(np.float32).astype(dtype).astype(np.float64)
    return np.moveaxis((codes * scale).reshape(v.shape), -1, axis)


WIDE = False


def mx_kscale(k):
    if not WIDE:
        return np.ones(k)
    levels = np.array([30, -30])
    if k % 512:
        return np.exp2(np.random.permutation(np.resize(levels, k // 32))).repeat(32)
    a = np.empty((k // 512, 16))
    for p in range(k // 512):
        a[p, :8] = np.random.permutation(np.resize(levels, 8))
        for g in range(8):
            far = levels[np.abs(levels - a[p, g]) >= 10]
            a[p, g + 8] = far[np.random.randint(len(far))]
    return np.exp2(a.ravel()).repeat(32)


BF16 = ml_dtypes.bfloat16


def bf(x):
    return np.asarray(x, np.float32).astype(BF16)


def f64(x):
    return np.asarray(x).astype(np.float64)


E2M1 = np.array([0.0, 0.5, 1.0, 1.5, 2.0, 3.0, 4.0, 6.0, -0.0, -0.5, -1.0, -1.5, -2.0, -3.0, -4.0, -6.0])


def pack_weight(w, fmt):
    k, n = w.shape
    w = f64(bf(w)).reshape(k // 32, 32, n)
    amax = np.abs(w).max(1)
    if fmt in ("e4m3", "e5m2"):
        byte = np.frexp(amax)[1] - 1 + 127 - (7 if fmt == "e4m3" else 14)
    else:
        mant, ex = np.frexp(amax / 6.0)
        byte = np.where(mant > 0.5, ex, ex - 1) + 127
    byte = np.clip(np.where(amax > 0, byte, 1), 1, 254)
    scaled = (w * np.exp2(127.0 - byte)[:, None, :]).reshape(k, n).astype(np.float32)
    by_word = np.ascontiguousarray(scaled.reshape(k // 512, 128, 4, n).transpose(0, 1, 3, 2))
    if fmt in ("e4m3", "e5m2"):
        words = by_word.astype(ml_dtypes.float8_e4m3fn if fmt == "e4m3" else ml_dtypes.float8_e5m2).view(np.uint8)
    else:
        c = by_word.astype(ml_dtypes.float4_e2m1fn).view(np.uint8) & 0xF
        words = c[..., 0::2] | (c[..., 1::2] << 4)
    return np.ascontiguousarray(words), np.ascontiguousarray(byte.astype(np.uint8).reshape(k // 512, 16, n))


def unpack_weight(words, scales, fmt):
    g, p, n, _ = words.shape
    if fmt in ("e4m3", "e5m2"):
        vals = np.ascontiguousarray(words).view(ml_dtypes.float8_e4m3fn if fmt == "e4m3" else ml_dtypes.float8_e5m2).astype(np.float64)
    else:
        nib = np.empty((g, p, n, 4), np.uint8)
        nib[..., 0::2] = words & 0xF
        nib[..., 1::2] = words >> 4
        vals = E2M1[nib]
    vals = vals * np.repeat(np.exp2(scales.astype(np.float64) - 127.0), 8, axis=1)[..., None]
    return vals.transpose(0, 1, 3, 2).reshape(g * 512, n)


T, D, R = 2560, 1024, 1536


def setup_inputs():
    s = mx_kscale(T)
    d = np.exp(0.3 * np.random.standard_normal(D))
    x = np.random.standard_normal((T, D)) * d
    G = np.random.standard_t(5, (T, R)) * np.sqrt(3 / 5) / np.sqrt(T)
    g_words, g_scales = pack_weight(G / s[:, None], "e5m2")
    return {"x": bf(x * s[:, None]),
            "g_words": g_words,
            "g_scales": g_scales,
            "c_prev": bf(np.random.standard_normal((D, R)) * d[:, None]),
            "inv_scale": bf(1 / d)}


def reference(x, g_words, g_scales, c_prev, inv_scale):
    xq = mxq(f64(x), 0, "e4m3")
    G = unpack_weight(g_words, g_scales, "e5m2")
    c = xq.T @ G
    z = (c + f64(c_prev)) * f64(inv_scale)[:, None]
    score = np.mean(np.square(z), axis=1)
    return z, score

@@ -1,0 +1,229 @@
+import math
+from contextlib import ExitStack
+
+import concourse.mybir as mybir
+
+T, D, R = 2560, 1024, 1536
+FLOPS = 2 * T * D * R
+
+F32 = mybir.dt.float32
+BF16 = mybir.dt.bfloat16
+I32 = mybir.dt.int32
+U32 = mybir.dt.uint32
+U8 = mybir.dt.uint8
+E4M3X4 = mybir.dt.float8_e4m3fn_x4
+E5M2X4 = mybir.dt.float8_e5m2_x4
+ACT = mybir.ActivationFunctionType
+ALU = mybir.AluOpType
+
+P = 128
+PACK = 4
+K_PASS = P * PACK
+PASSES = T // K_PASS
+N = 512
+D_TILES = D // P
+R_CHUNKS = R // N
+QUAD = 32
+
+
+def tile_residual_score_screen_e2_kernel(tc, x, g_words, g_scales, c_prev, inv_scale, out_0, out_1):
+    nc = tc.nc
+    last = PASSES - 1
+
+    with ExitStack() as ctx:
+        keep = ctx.enter_context(tc.tile_pool(name="keep", bufs=1))
+        stage = ctx.enter_context(tc.tile_pool(name="stage", bufs=4))
+        psum = ctx.enter_context(tc.psum_pool(name="psum", bufs=1))
+        ctx.enter_context(tc.manual_schedule())
+
+        words_hbm = g_words.rearrange("g p n t -> p g (n t)")
+
+        g_plane = [keep.tile([P, PASSES, N], U8, name="g_plane%d" % r, align_bytes=64) for r in range(R_CHUNKS)]
+        x_codes = [keep.tile([P, D], U32, name="x_codes%d" % g, align_bytes=64) for g in range(PASSES)]
+        x_plane = [keep.tile([P, D], U8, name="x_plane%d" % g, align_bytes=64) for g in range(PASSES)]
+        inv_rows = keep.tile([P, QUAD], BF16, name="inv_rows", align_bytes=64)
+        inv_turned = keep.tile([P, QUAD], BF16, name="inv_turned", align_bytes=64)
+        inv_col = keep.tile([P, D_TILES], F32, name="inv_col", align_bytes=64)
+        partial = keep.tile([P, D_TILES, 2], F32, name="partial", align_bytes=64)
+        score_col = keep.tile([P, QUAD], F32, name="score_col", align_bytes=64)
+        score_rows = keep.tile([P, QUAD], F32, name="score_rows", align_bytes=64)
+        z_front = [keep.tile([P, 2, 2 * N], F32, name="z_front%d" % a) for a in range(D_TILES // 2)]
+        z_back = [keep.tile([P, N], F32, name="z_back%d" % j) for j in range(D_TILES)]
+        squares = keep.tile([P, 2 * N], BF16, name="squares")
+
+        x_raw = {}
+        g_codes = {}
+        c_raw = {}
+
+        def load_x(g, c0, c1):
+            raw = keep.tile([P, PACK, c1 - c0], BF16, name="x_raw%d_%d" % (g, c0))
+            rows = x[g * K_PASS : (g + 1) * K_PASS, c0:c1]
+            nc.sync.dma_start(out=raw[:], in_=rows.rearrange("(p t) w -> p t w", t=PACK))
+            x_raw[(g, c0)] = raw
+
+        def load_g(r, g0, g1):
+            words = keep.tile([P, g1 - g0, N], U32, name="g_codes%d_%d" % (r, g0), align_bytes=64)
+            src = words_hbm[:, g0:g1, PACK * N * r : PACK * N * (r + 1)]
+            nc.sync.dma_start(out=words[:].bitcast(I32), in_=src.bitcast(I32))
+            for g in range(g0, g1):
+                g_codes[(r, g)] = words[:, g - g0, :]
+
+        def load_scales(r):
+            for s in range(4):
+                src = g_scales[:, s:16:4, N * r : N * (r + 1)].rearrange("g q n -> q g n")
+                nc.sync.dma_start(out=g_plane[r][s:P:QUAD, :, :].bitcast(I32), in_=src.bitcast(I32))
+
+        def load_c(a):
+            raw = keep.tile([P, 2, R], BF16, name="c_raw%d" % a)
+            rows = c_prev[2 * a * P : 2 * (a + 1) * P, :]
+            nc.sync.dma_start(out=raw[:], in_=rows.rearrange("(i p) n -> p i n", p=P))
+            c_raw[2 * a] = raw[:, 0, :]
+            c_raw[2 * a + 1] = raw[:, 1, :]
+
+        nc.gpsimd.memset(inv_rows[:], 0.0)
+        for q in range(4):
+            src = inv_scale.rearrange("(j q i) -> q j i", q=4, i=QUAD)[q]
+            nc.gpsimd.dma_start(out=inv_rows[QUAD * q : QUAD * q + D_TILES, :], in_=src)
+        for r in range(R_CHUNKS):
+            nc.vector.memset(g_plane[r][:].rearrange("p g n -> p (g n)").bitcast(I32), 0)
+        nc.vector.memset(score_col[:], 0.0)
+
+        load_x(0, 0, D)
+        load_x(1, 0, D)
+        load_scales(0)
+        load_g(0, 0, 1)
+        load_x(2, 0, D)
+        load_g(0, 1, 3)
+        load_x(3, 0, D)
+        load_g(0, 3, 5)
+        load_x(4, 0, D // 2)
+        load_x(4, D // 2, D)
+        load_scales(1)
+        load_g(1, 0, 2)
+        load_c(0)
+        load_g(1, 2, 5)
+        load_c(1)
+        load_c(2)
+        load_scales(2)
+        load_g(2, 0, 5)
+        load_c(3)
+
+        grouped = {}
+
+        def interleave(engine, g, c0, c1):
+            base = max(b for (gg, b) in x_raw if gg == g and b <= c0)
+            dst = stage.tile([P, c1 - c0, PACK], BF16, name="grouped", align_bytes=64)
+            src = x_raw[(g, base)][:, :, c0 - base : c1 - base].rearrange("p t w -> p w t")
+            if engine == "vector":
+                nc.vector.tensor_copy(out=dst[:], in_=src)
+            else:
+                nc.scalar.copy(out=dst[:], in_=src)
+            grouped[(g, c0)] = dst
+
+        def quantise(g, c0, c1):
+            nc.vector.quantize_mx(
+                out=x_codes[g][:, c0:c1].bitcast(E4M3X4),
+                scales=x_plane[g][:, c0:c1],
+                in_=grouped[(g, c0)][:].rearrange("p w t -> p (w t)"),
+            )
+
+        acc = {}
+
+        def multiply(j, r, g):
+            if g == 0:
+                acc[(j, r)] = psum.tile([P, N], F32, name="bank%d" % j)
+            cols = slice(j * P, (j + 1) * P)
+            nc.tensor.matmul_mx(
+                out=acc[(j, r)][:],
+                lhsT=x_codes[g][:, cols].bitcast(E4M3X4),
+                lhsT_scale=x_plane[g][:, cols],
+                rhs=g_codes[(r, g)].bitcast(E5M2X4),
+                rhs_scale=g_plane[r][:, g, :],
+                start=(g == 0),
+                stop=(g == last),
+            )
+
+        def z_of(j, r):
+            if r == R_CHUNKS - 1:
+                return z_back[j][:]
+            return z_front[j // 2][:, j % 2, r * N : (r + 1) * N]
+
+        half = D // 2
+        quarter = D // 4
+        for g in range(last):
+            interleave("vector", g, 0, half)
+            interleave("scalar", g, half, D)
+            if g > 0:
+                quantise(g - 1, half, D)
+                for j in range(D_TILES // 2, D_TILES):
+                    multiply(j, 0, g - 1)
+            else:
+                nc.vector.transpose(out=inv_turned[:], in_=inv_rows[:])
+            quantise(g, 0, half)
+            if g == 0:
+                nc.vector.tensor_copy(out=inv_col[:], in_=inv_turned[:, 0:D_TILES])
+            for j in range(D_TILES // 2):
+                multiply(j, 0, g)
+        quantise(last - 1, half, D)
+        for j in range(D_TILES // 2, D_TILES):
+            multiply(j, 0, last - 1)
+        interleave("vector", last, 0, quarter)
+        interleave("scalar", last, quarter, half)
+        interleave("vector", last, half, half + quarter)
+        interleave("scalar", last, half + quarter, D)
+        for u in range(4):
+            quantise(last, u * quarter, (u + 1) * quarter)
+            multiply(2 * u, 0, last)
+            multiply(2 * u + 1, 0, last)
+
+        for j in range(D_TILES):
+            if j % 2 == 0:
+                nc.scalar.activation(out=z_of(j, 0), in_=acc[(j, 0)][:], func=ACT.Copy, scale=inv_col[:, j : j + 1])
+            else:
+                nc.vector.tensor_scalar(
+                    out=z_of(j, 0), in0=acc[(j, 0)][:], scalar1=inv_col[:, j : j + 1], scalar2=None, op0=ALU.mult
+                )
+        for g in range(2):
+            for j in range(D_TILES):
+                multiply(j, 1, g)
+
+        def scale_c(j, r):
+            nc.vector.tensor_scalar(
+                out=z_of(j, r), in0=c_raw[j][:, r * N : (r + 1) * N], scalar1=inv_col[:, j : j + 1], scalar2=None,
+                op0=ALU.mult,
+            )
+
+        def finish(j, r, scaled):
+            nc.vector.scalar_tensor_tensor(
+                out=z_of(j, r), in0=scaled, scalar=inv_col[:, j : j + 1], in1=z_of(j, r), op0=ALU.mult, op1=ALU.add
+            )
+
+        def square(src, width, slot):
+            nc.scalar.activation(
+                out=squares[:, 0:width], in_=src, func=ACT.Square, scale=math.sqrt(1.0 / R), accum_out=slot
+            )
+
+        for j in range(D_TILES):
+            for g in range(2, PASSES):
+                multiply(j, 1, g)
+            scale_c(j, 1)
+            finish(j, 0, c_raw[j][:, 0:N])
+            scale_c(j, 2)
+            finish(j, 1, acc[(j, 1)][:])
+            square(z_front[j // 2][:, j % 2, :], 2 * N, partial[:, j, 0:1])
+            if j % 2 == 1:
+                rows = out_0[(j - 1) * P : (j + 1) * P, 0 : 2 * N]
+                nc.sync.dma_start(out=rows.rearrange("(i p) n -> p i n", p=P), in_=z_front[j // 2][:])
+
+        for j in range(D_TILES):
+            for g in range(PASSES):
+                multiply(j, 2, g)
+            finish(j, 2, acc[(j, 2)][:])
+            square(z_back[j][:], N, partial[:, j, 1:2])
+            nc.sync.dma_start(out=out_0[j * P : (j + 1) * P, 2 * N : R], in_=z_back[j][:])
+
+        nc.vector.tensor_reduce(out=score_col[:, 0:D_TILES], in_=partial[:], axis=mybir.AxisListType.X, op=ALU.add)
+        nc.vector.transpose(out=score_rows[:], in_=score_col[:])
+        for q in range(4):
+            dst = out_1.rearrange("(j q i) -> q j i", q=4, i=QUAD)[q]
+            nc.scalar.dma_start(out=dst, in_=score_rows[QUAD * q : QUAD * q + D_TILES, :])

@@ -44,12 +44,11 @@ def tile_residual_score_screen_e2_kernel(tc, x, g_words, g_scales, c_prev, inv_s
         inv_rows = keep.tile([P, QUAD], BF16, name="inv_rows", align_bytes=64)
         inv_turned = keep.tile([P, QUAD], BF16, name="inv_turned", align_bytes=64)
         inv_col = keep.tile([P, D_TILES], F32, name="inv_col", align_bytes=64)
-        partial = keep.tile([P, D_TILES, 2], F32, name="partial", align_bytes=64)
+        partial = keep.tile([P, D_TILES, 3], F32, name="partial", align_bytes=64)
         score_col = keep.tile([P, QUAD], F32, name="score_col", align_bytes=64)
         score_rows = keep.tile([P, QUAD], F32, name="score_rows", align_bytes=64)
         z_front = [keep.tile([P, 2, 2 * N], F32, name="z_front%d" % a) for a in range(D_TILES // 2)]
         z_back = [keep.tile([P, N], F32, name="z_back%d" % j) for j in range(D_TILES)]
-        squares = keep.tile([P, 2 * N], BF16, name="squares")
 
         x_raw = {}
         g_codes = {}
@@ -80,13 +79,11 @@ def tile_residual_score_screen_e2_kernel(tc, x, g_words, g_scales, c_prev, inv_s
             c_raw[2 * a] = raw[:, 0, :]
             c_raw[2 * a + 1] = raw[:, 1, :]
 
-        nc.gpsimd.memset(inv_rows[:], 0.0)
-        for q in range(4):
-            src = inv_scale.rearrange("(j q i) -> q j i", q=4, i=QUAD)[q]
-            nc.gpsimd.dma_start(out=inv_rows[QUAD * q : QUAD * q + D_TILES, :], in_=src)
         for r in range(R_CHUNKS):
             nc.vector.memset(g_plane[r][:].rearrange("p g n -> p (g n)").bitcast(I32), 0)
+        nc.vector.memset(inv_rows[:], 0.0)
         nc.vector.memset(score_col[:], 0.0)
+        nc.vector.memset(partial[:], 0.0)
 
         load_x(0, 0, D)
         load_x(1, 0, D)
@@ -94,6 +91,9 @@ def tile_residual_score_screen_e2_kernel(tc, x, g_words, g_scales, c_prev, inv_s
         load_g(0, 0, 1)
         load_x(2, 0, D)
         load_g(0, 1, 3)
+        for q in range(4):
+            src = inv_scale.rearrange("(j q i) -> q j i", q=4, i=QUAD)[q]
+            nc.sync.dma_start(out=inv_rows[QUAD * q : QUAD * q + D_TILES, :], in_=src)
         load_x(3, 0, D)
         load_g(0, 3, 5)
         load_x(4, 0, D // 2)
@@ -157,10 +157,10 @@ def tile_residual_score_screen_e2_kernel(tc, x, g_words, g_scales, c_prev, inv_s
                 quantise(g - 1, half, D)
                 for j in range(D_TILES // 2, D_TILES):
                     multiply(j, 0, g - 1)
-            else:
+            if g == last - 1:
                 nc.vector.transpose(out=inv_turned[:], in_=inv_rows[:])
             quantise(g, 0, half)
-            if g == 0:
+            if g == last - 1:
                 nc.vector.tensor_copy(out=inv_col[:], in_=inv_turned[:, 0:D_TILES])
             for j in range(D_TILES // 2):
                 multiply(j, 0, g)
@@ -199,6 +199,7 @@ def tile_residual_score_screen_e2_kernel(tc, x, g_words, g_scales, c_prev, inv_s
             )
 
         def square(src, width, slot):
+            squares = stage.tile([P, 2 * N], BF16, name="squares", bufs=2)
             nc.scalar.activation(
                 out=squares[:, 0:width], in_=src, func=ACT.Square, scale=math.sqrt(1.0 / R), accum_out=slot
             )
@@ -218,12 +219,21 @@ def tile_residual_score_screen_e2_kernel(tc, x, g_words, g_scales, c_prev, inv_s
         for j in range(D_TILES):
             for g in range(PASSES):
                 multiply(j, 2, g)
-            finish(j, 2, acc[(j, 2)][:])
-            square(z_back[j][:], N, partial[:, j, 1:2])
+            pieces = 2 if j == D_TILES - 1 else 1
+            width = N // pieces
+            for u in range(pieces):
+                cols = slice(u * width, (u + 1) * width)
+                nc.vector.scalar_tensor_tensor(
+                    out=z_back[j][:, cols], in0=acc[(j, 2)][:, cols], scalar=inv_col[:, j : j + 1],
+                    in1=z_back[j][:, cols], op0=ALU.mult, op1=ALU.add,
+                )
+            for u in range(pieces):
+                square(z_back[j][:, u * width : (u + 1) * width], width, partial[:, j, 1 + u : 2 + u])
             nc.sync.dma_start(out=out_0[j * P : (j + 1) * P, 2 * N : R], in_=z_back[j][:])
 
         nc.vector.tensor_reduce(out=score_col[:, 0:D_TILES], in_=partial[:], axis=mybir.AxisListType.X, op=ALU.add)
         nc.vector.transpose(out=score_rows[:], in_=score_col[:])
         for q in range(4):
             dst = out_1.rearrange("(j q i) -> q j i", q=4, i=QUAD)[q]
-            nc.scalar.dma_start(out=dst, in_=score_rows[QUAD * q : QUAD * q + D_TILES, :])
+            queue = nc.scalar if q % 2 == 0 else nc.sync
+            queue.dma_start(out=dst, in_=score_rows[QUAD * q : QUAD * q + D_TILES, :])

@@ -2,6 +2,7 @@ import math
 from contextlib import ExitStack
 
 import concourse.mybir as mybir
+from concourse.masks import make_identity
 
 T, D, R = 2560, 1024, 1536
 FLOPS = 2 * T * D * R
@@ -29,6 +30,9 @@ QUAD = 32
 def tile_residual_score_screen_e2_kernel(tc, x, g_words, g_scales, c_prev, inv_scale, out_0, out_1):
     nc = tc.nc
     last = PASSES - 1
+    half = D // 2
+    quarter = D // 4
+    group = D_TILES // 2
 
     with ExitStack() as ctx:
         keep = ctx.enter_context(tc.tile_pool(name="keep", bufs=1))
@@ -38,17 +42,24 @@ def tile_residual_score_screen_e2_kernel(tc, x, g_words, g_scales, c_prev, inv_s
 
         words_hbm = g_words.rearrange("g p n t -> p g (n t)")
 
-        g_plane = [keep.tile([P, PASSES, N], U8, name="g_plane%d" % r, align_bytes=64) for r in range(R_CHUNKS)]
+        plane_first = keep.tile([P, PASSES, N], U8, name="plane_first", align_bytes=64)
+        plane_rest = keep.tile([P, PASSES, 2 * N], U8, name="plane_rest", align_bytes=64)
         x_codes = [keep.tile([P, D], U32, name="x_codes%d" % g, align_bytes=64) for g in range(PASSES)]
         x_plane = [keep.tile([P, D], U8, name="x_plane%d" % g, align_bytes=64) for g in range(PASSES)]
-        inv_rows = keep.tile([P, QUAD], BF16, name="inv_rows", align_bytes=64)
-        inv_turned = keep.tile([P, QUAD], BF16, name="inv_turned", align_bytes=64)
-        inv_col = keep.tile([P, D_TILES], F32, name="inv_col", align_bytes=64)
-        partial = keep.tile([P, D_TILES, 3], F32, name="partial", align_bytes=64)
-        score_col = keep.tile([P, QUAD], F32, name="score_col", align_bytes=64)
-        score_rows = keep.tile([P, QUAD], F32, name="score_rows", align_bytes=64)
-        z_front = [keep.tile([P, 2, 2 * N], F32, name="z_front%d" % a) for a in range(D_TILES // 2)]
-        z_back = [keep.tile([P, N], F32, name="z_back%d" % j) for j in range(D_TILES)]
+        ident_bf = keep.tile([P, P], BF16, name="ident_bf")
+        ident_f32 = keep.tile([P, P], F32, name="ident_f32")
+        inv_rows = keep.tile([P, P], BF16, name="inv_rows")
+        inv_col = keep.tile([P, D_TILES], F32, name="inv_col")
+        partial = [keep.tile([P, P], F32, name="partial%d" % s) for s in range(3)]
+        score_rows = keep.tile([D_TILES, P], F32, name="score_rows")
+        z_front = [keep.tile([P, group, 2 * N], F32, name="z_front%d" % a) for a in range(2)]
+        back_spans = [(0, 4), (4, 6), (6, 7), (7, 8)]
+        z_back = {}
+        back_tile = {}
+        for j0, j1 in back_spans:
+            back_tile[j1 - 1] = keep.tile([P, j1 - j0, N], F32, name="z_back%d" % j0)
+            for j in range(j0, j1):
+                z_back[j] = back_tile[j1 - 1][:, j - j0, :]
 
         x_raw = {}
         g_codes = {}
@@ -67,46 +78,53 @@ def tile_residual_score_screen_e2_kernel(tc, x, g_words, g_scales, c_prev, inv_s
             for g in range(g0, g1):
                 g_codes[(r, g)] = words[:, g - g0, :]
 
-        def load_scales(r):
+        def load_scales(plane, n0, n1):
             for s in range(4):
-                src = g_scales[:, s:16:4, N * r : N * (r + 1)].rearrange("g q n -> q g n")
-                nc.sync.dma_start(out=g_plane[r][s:P:QUAD, :, :].bitcast(I32), in_=src.bitcast(I32))
+                src = g_scales[:, s:16:4, n0:n1].rearrange("g q n -> q g n")
+                nc.sync.dma_start(out=plane[s:P:QUAD, :, :].bitcast(I32), in_=src.bitcast(I32))
 
-        def load_c(a):
-            raw = keep.tile([P, 2, R], BF16, name="c_raw%d" % a)
-            rows = c_prev[2 * a * P : 2 * (a + 1) * P, :]
+        def g_scale(r, g):
+            if r == 0:
+                return plane_first[:, g, :]
+            return plane_rest[:, g, (r - 1) * N : r * N]
+
+        def load_c(j0, j1, r0, r1):
+            raw = keep.tile([P, j1 - j0, (r1 - r0) * N], BF16, name="c_raw%d_%d" % (j0, r0))
+            rows = c_prev[j0 * P : j1 * P, r0 * N : r1 * N]
             nc.sync.dma_start(out=raw[:], in_=rows.rearrange("(i p) n -> p i n", p=P))
-            c_raw[2 * a] = raw[:, 0, :]
-            c_raw[2 * a + 1] = raw[:, 1, :]
+            for j in range(j0, j1):
+                for r in range(r0, r1):
+                    c_raw[(j, r)] = raw[:, j - j0, (r - r0) * N : (r - r0 + 1) * N]
 
-        for r in range(R_CHUNKS):
-            nc.vector.memset(g_plane[r][:].rearrange("p g n -> p (g n)").bitcast(I32), 0)
         nc.vector.memset(inv_rows[:], 0.0)
-        nc.vector.memset(score_col[:], 0.0)
-        nc.vector.memset(partial[:], 0.0)
+        nc.vector.memset(plane_first[:].rearrange("p g n -> p (g n)").bitcast(I32), 0)
+        nc.vector.memset(plane_rest[:].rearrange("p g n -> p (g n)").bitcast(I32), 0)
+        for s in range(3):
+            nc.vector.memset(partial[s][:], 0.0)
+        make_identity(nc, ident_bf[:])
+        make_identity(nc, ident_f32[:])
 
         load_x(0, 0, D)
+        nc.scalar.dma_start(out=inv_rows[0:D_TILES, :], in_=inv_scale.rearrange("(j p) -> j p", p=P))
         load_x(1, 0, D)
-        load_scales(0)
+        load_scales(plane_first, 0, N)
         load_g(0, 0, 1)
         load_x(2, 0, D)
         load_g(0, 1, 3)
-        for q in range(4):
-            src = inv_scale.rearrange("(j q i) -> q j i", q=4, i=QUAD)[q]
-            nc.sync.dma_start(out=inv_rows[QUAD * q : QUAD * q + D_TILES, :], in_=src)
         load_x(3, 0, D)
         load_g(0, 3, 5)
-        load_x(4, 0, D // 2)
-        load_x(4, D // 2, D)
-        load_scales(1)
+        load_x(4, 0, half)
+        load_x(4, half, D)
+        load_scales(plane_rest, N, R)
         load_g(1, 0, 2)
-        load_c(0)
+        load_c(0, group, 0, 2)
         load_g(1, 2, 5)
-        load_c(1)
-        load_c(2)
-        load_scales(2)
+        load_c(group, D_TILES, 0, 2)
         load_g(2, 0, 5)
-        load_c(3)
+        load_c(0, D_TILES, 2, 3)
+
+        inv_turned = psum.tile([P, P], BF16, name="bank%d" % (D_TILES - 1))
+        nc.tensor.transpose(inv_turned[:], inv_rows[:], ident_bf[:])
 
         grouped = {}
 
@@ -138,34 +156,30 @@ def tile_residual_score_screen_e2_kernel(tc, x, g_words, g_scales, c_prev, inv_s
                 lhsT=x_codes[g][:, cols].bitcast(E4M3X4),
                 lhsT_scale=x_plane[g][:, cols],
                 rhs=g_codes[(r, g)].bitcast(E5M2X4),
-                rhs_scale=g_plane[r][:, g, :],
+                rhs_scale=g_scale(r, g),
                 start=(g == 0),
                 stop=(g == last),
             )
 
         def z_of(j, r):
             if r == R_CHUNKS - 1:
-                return z_back[j][:]
-            return z_front[j // 2][:, j % 2, r * N : (r + 1) * N]
+                return z_back[j]
+            return z_front[j // group][:, j % group, r * N : (r + 1) * N]
 
-        half = D // 2
-        quarter = D // 4
         for g in range(last):
             interleave("vector", g, 0, half)
             interleave("scalar", g, half, D)
             if g > 0:
                 quantise(g - 1, half, D)
-                for j in range(D_TILES // 2, D_TILES):
+                for j in range(group, D_TILES):
                     multiply(j, 0, g - 1)
-            if g == last - 1:
-                nc.vector.transpose(out=inv_turned[:], in_=inv_rows[:])
-            quantise(g, 0, half)
-            if g == last - 1:
+            else:
                 nc.vector.tensor_copy(out=inv_col[:], in_=inv_turned[:, 0:D_TILES])
-            for j in range(D_TILES // 2):
+            quantise(g, 0, half)
+            for j in range(group):
                 multiply(j, 0, g)
         quantise(last - 1, half, D)
-        for j in range(D_TILES // 2, D_TILES):
+        for j in range(group, D_TILES):
             multiply(j, 0, last - 1)
         interleave("vector", last, 0, quarter)
         interleave("scalar", last, quarter, half)
@@ -189,13 +203,12 @@ def tile_residual_score_screen_e2_kernel(tc, x, g_words, g_scales, c_prev, inv_s
 
         def scale_c(j, r):
             nc.vector.tensor_scalar(
-                out=z_of(j, r), in0=c_raw[j][:, r * N : (r + 1) * N], scalar1=inv_col[:, j : j + 1], scalar2=None,
-                op0=ALU.mult,
+                out=z_of(j, r), in0=c_raw[(j, r)], scalar1=inv_col[:, j : j + 1], scalar2=None, op0=ALU.mult
             )
 
-        def finish(j, r, scaled):
+        def finish(j, z, unscaled):
             nc.vector.scalar_tensor_tensor(
-                out=z_of(j, r), in0=scaled, scalar=inv_col[:, j : j + 1], in1=z_of(j, r), op0=ALU.mult, op1=ALU.add
+                out=z, in0=unscaled, scalar=inv_col[:, j : j + 1], in1=z, op0=ALU.mult, op1=ALU.add
             )
 
         def square(src, width, slot):
@@ -208,32 +221,35 @@ def tile_residual_score_screen_e2_kernel(tc, x, g_words, g_scales, c_prev, inv_s
             for g in range(2, PASSES):
                 multiply(j, 1, g)
             scale_c(j, 1)
-            finish(j, 0, c_raw[j][:, 0:N])
-            scale_c(j, 2)
-            finish(j, 1, acc[(j, 1)][:])
-            square(z_front[j // 2][:, j % 2, :], 2 * N, partial[:, j, 0:1])
-            if j % 2 == 1:
-                rows = out_0[(j - 1) * P : (j + 1) * P, 0 : 2 * N]
-                nc.sync.dma_start(out=rows.rearrange("(i p) n -> p i n", p=P), in_=z_front[j // 2][:])
+            finish(j, z_of(j, 0), c_raw[(j, 0)])
+            finish(j, z_of(j, 1), acc[(j, 1)][:])
+            square(z_front[j // group][:, j % group, :], 2 * N, partial[0][:, j : j + 1])
+            if j % group == group - 1:
+                rows = out_0[(j + 1 - group) * P : (j + 1) * P, 0 : 2 * N]
+                nc.sync.dma_start(out=rows.rearrange("(i p) n -> p i n", p=P), in_=z_front[j // group][:])
 
+        scale_c(0, 2)
         for j in range(D_TILES):
             for g in range(PASSES):
                 multiply(j, 2, g)
+            if j + 1 < D_TILES:
+                scale_c(j + 1, 2)
             pieces = 2 if j == D_TILES - 1 else 1
             width = N // pieces
             for u in range(pieces):
                 cols = slice(u * width, (u + 1) * width)
-                nc.vector.scalar_tensor_tensor(
-                    out=z_back[j][:, cols], in0=acc[(j, 2)][:, cols], scalar=inv_col[:, j : j + 1],
-                    in1=z_back[j][:, cols], op0=ALU.mult, op1=ALU.add,
-                )
+                finish(j, z_back[j][:, cols], acc[(j, 2)][:, cols])
             for u in range(pieces):
-                square(z_back[j][:, u * width : (u + 1) * width], width, partial[:, j, 1 + u : 2 + u])
-            nc.sync.dma_start(out=out_0[j * P : (j + 1) * P, 2 * N : R], in_=z_back[j][:])
+                square(z_back[j][:, u * width : (u + 1) * width], width, partial[1 + u][:, j : j + 1])
+            if j in back_tile:
+                count = back_tile[j].shape[1]
+                rows = out_0[(j + 1 - count) * P : (j + 1) * P, 2 * N : R]
+                nc.sync.dma_start(out=rows.rearrange("(i p) n -> p i n", p=P), in_=back_tile[j][:])
 
-        nc.vector.tensor_reduce(out=score_col[:, 0:D_TILES], in_=partial[:], axis=mybir.AxisListType.X, op=ALU.add)
-        nc.vector.transpose(out=score_rows[:], in_=score_col[:])
-        for q in range(4):
-            dst = out_1.rearrange("(j q i) -> q j i", q=4, i=QUAD)[q]
-            queue = nc.scalar if q % 2 == 0 else nc.sync
-            queue.dma_start(out=dst, in_=score_rows[QUAD * q : QUAD * q + D_TILES, :])
+        score_turned = psum.tile([P, P], F32, name="bank0")
+        for s in range(3):
+            nc.tensor.matmul(
+                score_turned[:], lhsT=partial[s][:], rhs=ident_f32[:], is_transpose=True, start=(s == 0), stop=(s == 2)
+            )
+        nc.vector.tensor_copy(out=score_rows[:], in_=score_turned[0:D_TILES, :])
+        nc.scalar.dma_start(out=out_1.rearrange("(j p) -> j p", p=P), in_=score_rows[:])

@@ -42,8 +42,7 @@ def tile_residual_score_screen_e2_kernel(tc, x, g_words, g_scales, c_prev, inv_s
 
         words_hbm = g_words.rearrange("g p n t -> p g (n t)")
 
-        plane_first = keep.tile([P, PASSES, N], U8, name="plane_first", align_bytes=64)
-        plane_rest = keep.tile([P, PASSES, 2 * N], U8, name="plane_rest", align_bytes=64)
+        g_plane = [keep.tile([P, PASSES, N], U8, name="g_plane%d" % r, align_bytes=64) for r in range(R_CHUNKS)]
         x_codes = [keep.tile([P, D], U32, name="x_codes%d" % g, align_bytes=64) for g in range(PASSES)]
         x_plane = [keep.tile([P, D], U8, name="x_plane%d" % g, align_bytes=64) for g in range(PASSES)]
         ident_bf = keep.tile([P, P], BF16, name="ident_bf")
@@ -78,15 +77,10 @@ def tile_residual_score_screen_e2_kernel(tc, x, g_words, g_scales, c_prev, inv_s
             for g in range(g0, g1):
                 g_codes[(r, g)] = words[:, g - g0, :]
 
-        def load_scales(plane, n0, n1):
+        def load_scales(r):
             for s in range(4):
-                src = g_scales[:, s:16:4, n0:n1].rearrange("g q n -> q g n")
-                nc.sync.dma_start(out=plane[s:P:QUAD, :, :].bitcast(I32), in_=src.bitcast(I32))
-
-        def g_scale(r, g):
-            if r == 0:
-                return plane_first[:, g, :]
-            return plane_rest[:, g, (r - 1) * N : r * N]
+                src = g_scales[:, s:16:4, N * r : N * (r + 1)].rearrange("g q n -> q g n")
+                nc.sync.dma_start(out=g_plane[r][s:P:QUAD, :, :].bitcast(I32), in_=src.bitcast(I32))
 
         def load_c(j0, j1, r0, r1):
             raw = keep.tile([P, j1 - j0, (r1 - r0) * N], BF16, name="c_raw%d_%d" % (j0, r0))
@@ -97,8 +91,8 @@ def tile_residual_score_screen_e2_kernel(tc, x, g_words, g_scales, c_prev, inv_s
                     c_raw[(j, r)] = raw[:, j - j0, (r - r0) * N : (r - r0 + 1) * N]
 
         nc.vector.memset(inv_rows[:], 0.0)
-        nc.vector.memset(plane_first[:].rearrange("p g n -> p (g n)").bitcast(I32), 0)
-        nc.vector.memset(plane_rest[:].rearrange("p g n -> p (g n)").bitcast(I32), 0)
+        for r in range(R_CHUNKS):
+            nc.vector.memset(g_plane[r][:].rearrange("p g n -> p (g n)").bitcast(I32), 0)
         for s in range(3):
             nc.vector.memset(partial[s][:], 0.0)
         make_identity(nc, ident_bf[:])
@@ -106,20 +100,21 @@ def tile_residual_score_screen_e2_kernel(tc, x, g_words, g_scales, c_prev, inv_s
 
         load_x(0, 0, D)
         nc.scalar.dma_start(out=inv_rows[0:D_TILES, :], in_=inv_scale.rearrange("(j p) -> j p", p=P))
-        load_x(1, 0, D)
-        load_scales(plane_first, 0, N)
+        load_scales(0)
         load_g(0, 0, 1)
-        load_x(2, 0, D)
+        load_x(1, 0, D)
         load_g(0, 1, 3)
+        load_x(2, 0, D)
         load_x(3, 0, D)
         load_g(0, 3, 5)
         load_x(4, 0, half)
         load_x(4, half, D)
-        load_scales(plane_rest, N, R)
+        load_scales(1)
         load_g(1, 0, 2)
         load_c(0, group, 0, 2)
         load_g(1, 2, 5)
         load_c(group, D_TILES, 0, 2)
+        load_scales(2)
         load_g(2, 0, 5)
         load_c(0, D_TILES, 2, 3)
 
@@ -131,11 +126,12 @@ def tile_residual_score_screen_e2_kernel(tc, x, g_words, g_scales, c_prev, inv_s
         def interleave(engine, g, c0, c1):
             base = max(b for (gg, b) in x_raw if gg == g and b <= c0)
             dst = stage.tile([P, c1 - c0, PACK], BF16, name="grouped", align_bytes=64)
-            src = x_raw[(g, base)][:, :, c0 - base : c1 - base].rearrange("p t w -> p w t")
+            src = x_raw[(g, base)][:, :, c0 - base : c1 - base].rearrange("p t (c i) -> p c t i", i=4)
+            walk = dst[:].rearrange("p (c i) t -> p c t i", i=4)
             if engine == "vector":
-                nc.vector.tensor_copy(out=dst[:], in_=src)
+                nc.vector.tensor_copy(out=walk, in_=src)
             else:
-                nc.scalar.copy(out=dst[:], in_=src)
+                nc.scalar.copy(out=walk, in_=src)
             grouped[(g, c0)] = dst
 
         def quantise(g, c0, c1):
@@ -156,7 +152,7 @@ def tile_residual_score_screen_e2_kernel(tc, x, g_words, g_scales, c_prev, inv_s
                 lhsT=x_codes[g][:, cols].bitcast(E4M3X4),
                 lhsT_scale=x_plane[g][:, cols],
                 rhs=g_codes[(r, g)].bitcast(E5M2X4),
-                rhs_scale=g_scale(r, g),
+                rhs_scale=g_plane[r][:, g, :],
                 start=(g == 0),
                 stop=(g == last),
             )
@@ -217,12 +213,19 @@ def tile_residual_score_screen_e2_kernel(tc, x, g_words, g_scales, c_prev, inv_s
                 out=squares[:, 0:width], in_=src, func=ACT.Square, scale=math.sqrt(1.0 / R), accum_out=slot
             )
 
+        def prepare(j):
+            scale_c(j, 1)
+            finish(j, z_of(j, 0), c_raw[(j, 0)])
+
+        ahead = 3
+        for j in range(ahead):
+            prepare(j)
         for j in range(D_TILES):
             for g in range(2, PASSES):
                 multiply(j, 1, g)
-            scale_c(j, 1)
-            finish(j, z_of(j, 0), c_raw[(j, 0)])
             finish(j, z_of(j, 1), acc[(j, 1)][:])
+            if j + ahead < D_TILES:
+                prepare(j + ahead)
             square(z_front[j // group][:, j % group, :], 2 * N, partial[0][:, j : j + 1])
             if j % group == group - 1:
                 rows = out_0[(j + 1 - group) * P : (j + 1) * P, 0 : 2 * N]
@@ -234,13 +237,16 @@ def tile_residual_score_screen_e2_kernel(tc, x, g_words, g_scales, c_prev, inv_s
                 multiply(j, 2, g)
             if j + 1 < D_TILES:
                 scale_c(j + 1, 2)
-            pieces = 2 if j == D_TILES - 1 else 1
-            width = N // pieces
-            for u in range(pieces):
-                cols = slice(u * width, (u + 1) * width)
-                finish(j, z_back[j][:, cols], acc[(j, 2)][:, cols])
-            for u in range(pieces):
-                square(z_back[j][:, u * width : (u + 1) * width], width, partial[1 + u][:, j : j + 1])
+            width = N if j + 1 < D_TILES else 320
+            finish(j, z_back[j][:, 0:width], acc[(j, 2)][:, 0:width])
+            square(z_back[j][:, 0:width], width, partial[1][:, j : j + 1])
+            if width < N:
+                finish(j, z_back[j][:, width:N], acc[(j, 2)][:, width:N])
+                squares_end = keep.tile([P, N - width], F32, name="squares_end")
+                nc.vector.scalar_tensor_tensor(
+                    out=squares_end[:], in0=z_back[j][:, width:N], scalar=1.0 / R, in1=z_back[j][:, width:N],
+                    op0=ALU.mult, op1=ALU.mult, accum_out=partial[2][:, j : j + 1],
+                )
             if j in back_tile:
                 count = back_tile[j].shape[1]
                 rows = out_0[(j + 1 - count) * P : (j + 1) * P, 2 * N : R]

@@ -21,26 +21,30 @@ P = 128
 PACK = 4
 K_PASS = P * PACK
 PASSES = T // K_PASS
+BLOCKS = K_PASS // 32
+LAST_PASS = PASSES - 1
 N = 512
 D_TILES = D // P
+HALF_TILES = D_TILES // 2
 R_CHUNKS = R // N
-QUAD = 32
+LAST_CHUNK = R_CHUNKS - 1
+QUADRANT = 32
+SCALE_ROWS = 4
+HALF = D // 2
+QUARTER = D // 4
+RUN = 4
+LAST_CHUNK_STORES = [(0, 4), (4, 6), (6, 7), (7, 8)]
+TAIL_SPLIT = 384
 
 
 def tile_residual_score_screen_e2_kernel(tc, x, g_words, g_scales, c_prev, inv_scale, out_0, out_1):
     nc = tc.nc
-    last = PASSES - 1
-    half = D // 2
-    quarter = D // 4
-    group = D_TILES // 2
 
     with ExitStack() as ctx:
         keep = ctx.enter_context(tc.tile_pool(name="keep", bufs=1))
-        stage = ctx.enter_context(tc.tile_pool(name="stage", bufs=4))
+        stage = ctx.enter_context(tc.tile_pool(name="stage", bufs=1))
         psum = ctx.enter_context(tc.psum_pool(name="psum", bufs=1))
         ctx.enter_context(tc.manual_schedule())
-
-        words_hbm = g_words.rearrange("g p n t -> p g (n t)")
 
         g_plane = [keep.tile([P, PASSES, N], U8, name="g_plane%d" % r, align_bytes=64) for r in range(R_CHUNKS)]
         x_codes = [keep.tile([P, D], U32, name="x_codes%d" % g, align_bytes=64) for g in range(PASSES)]
@@ -49,17 +53,28 @@ def tile_residual_score_screen_e2_kernel(tc, x, g_words, g_scales, c_prev, inv_s
         ident_f32 = keep.tile([P, P], F32, name="ident_f32")
         inv_rows = keep.tile([P, P], BF16, name="inv_rows")
         inv_col = keep.tile([P, D_TILES], F32, name="inv_col")
-        partial = [keep.tile([P, P], F32, name="partial%d" % s) for s in range(3)]
+        share_front = keep.tile([P, P], F32, name="share_front")
+        share_back = keep.tile([P, P], F32, name="share_back")
+        share_tail = keep.tile([P, P], F32, name="share_tail")
+        shares = [share_front, share_back, share_tail]
         score_rows = keep.tile([D_TILES, P], F32, name="score_rows")
-        z_front = [keep.tile([P, group, 2 * N], F32, name="z_front%d" % a) for a in range(2)]
-        back_spans = [(0, 4), (4, 6), (6, 7), (7, 8)]
+        z_front = [keep.tile([P, HALF_TILES, 2 * N], F32, name="z_front%d" % a) for a in range(2)]
         z_back = {}
-        back_tile = {}
-        for j0, j1 in back_spans:
-            back_tile[j1 - 1] = keep.tile([P, j1 - j0, N], F32, name="z_back%d" % j0)
+        back_store = {}
+        for j0, j1 in LAST_CHUNK_STORES:
+            back_store[j1 - 1] = keep.tile([P, j1 - j0, N], F32, name="z_back%d" % j0)
             for j in range(j0, j1):
-                z_back[j] = back_tile[j1 - 1][:, j - j0, :]
+                z_back[j] = back_store[j1 - 1][:, j - j0, :]
 
+        def z_of(j, r):
+            if r == LAST_CHUNK:
+                return z_back[j]
+            return z_front[j // HALF_TILES][:, j % HALF_TILES, r * N : (r + 1) * N]
+
+        def inv_of(j):
+            return inv_col[:, j : j + 1]
+
+        words_hbm = g_words.rearrange("g p n t -> p g (n t)")
         x_raw = {}
         g_codes = {}
         c_raw = {}
@@ -78,9 +93,9 @@ def tile_residual_score_screen_e2_kernel(tc, x, g_words, g_scales, c_prev, inv_s
                 g_codes[(r, g)] = words[:, g - g0, :]
 
         def load_scales(r):
-            for s in range(4):
-                src = g_scales[:, s:16:4, N * r : N * (r + 1)].rearrange("g q n -> q g n")
-                nc.sync.dma_start(out=g_plane[r][s:P:QUAD, :, :].bitcast(I32), in_=src.bitcast(I32))
+            for s in range(SCALE_ROWS):
+                src = g_scales[:, s:BLOCKS:SCALE_ROWS, N * r : N * (r + 1)].rearrange("g q n -> q g n")
+                nc.sync.dma_start(out=g_plane[r][s:P:QUADRANT, :, :].bitcast(I32), in_=src.bitcast(I32))
 
         def load_c(j0, j1, r0, r1):
             raw = keep.tile([P, j1 - j0, (r1 - r0) * N], BF16, name="c_raw%d_%d" % (j0, r0))
@@ -93,8 +108,8 @@ def tile_residual_score_screen_e2_kernel(tc, x, g_words, g_scales, c_prev, inv_s
         nc.vector.memset(inv_rows[:], 0.0)
         for r in range(R_CHUNKS):
             nc.vector.memset(g_plane[r][:].rearrange("p g n -> p (g n)").bitcast(I32), 0)
-        for s in range(3):
-            nc.vector.memset(partial[s][:], 0.0)
+        for share in shares:
+            nc.vector.memset(share[:], 0.0)
         make_identity(nc, ident_bf[:])
         make_identity(nc, ident_f32[:])
 
@@ -102,46 +117,33 @@ def tile_residual_score_screen_e2_kernel(tc, x, g_words, g_scales, c_prev, inv_s
         nc.scalar.dma_start(out=inv_rows[0:D_TILES, :], in_=inv_scale.rearrange("(j p) -> j p", p=P))
         load_scales(0)
         load_g(0, 0, 1)
-        load_x(1, 0, D)
-        load_g(0, 1, 3)
-        load_x(2, 0, D)
-        load_x(3, 0, D)
-        load_g(0, 3, 5)
-        load_x(4, 0, half)
-        load_x(4, half, D)
+        for g in range(1, LAST_PASS):
+            load_x(g, 0, D)
+            load_g(0, g, g + 1)
+        load_x(LAST_PASS, 0, HALF)
+        load_g(0, LAST_PASS, PASSES)
+        load_x(LAST_PASS, HALF, D)
         load_scales(1)
-        load_g(1, 0, 2)
-        load_c(0, group, 0, 2)
-        load_g(1, 2, 5)
-        load_c(group, D_TILES, 0, 2)
-        load_scales(2)
-        load_g(2, 0, 5)
-        load_c(0, D_TILES, 2, 3)
+        load_g(1, 0, 1)
+        load_g(1, 1, PASSES)
+        load_c(0, HALF_TILES, 0, LAST_CHUNK)
+        load_c(HALF_TILES, D_TILES, 0, LAST_CHUNK)
+        load_scales(LAST_CHUNK)
+        load_g(LAST_CHUNK, 0, PASSES)
+        load_c(0, D_TILES, LAST_CHUNK, R_CHUNKS)
 
         inv_turned = psum.tile([P, P], BF16, name="bank%d" % (D_TILES - 1))
         nc.tensor.transpose(inv_turned[:], inv_rows[:], ident_bf[:])
 
         grouped = {}
-
-        def interleave(engine, g, c0, c1):
-            base = max(b for (gg, b) in x_raw if gg == g and b <= c0)
-            dst = stage.tile([P, c1 - c0, PACK], BF16, name="grouped", align_bytes=64)
-            src = x_raw[(g, base)][:, :, c0 - base : c1 - base].rearrange("p t (c i) -> p c t i", i=4)
-            walk = dst[:].rearrange("p (c i) t -> p c t i", i=4)
-            if engine == "vector":
-                nc.vector.tensor_copy(out=walk, in_=src)
-            else:
-                nc.scalar.copy(out=walk, in_=src)
-            grouped[(g, c0)] = dst
-
-        def quantise(g, c0, c1):
-            nc.vector.quantize_mx(
-                out=x_codes[g][:, c0:c1].bitcast(E4M3X4),
-                scales=x_plane[g][:, c0:c1],
-                in_=grouped[(g, c0)][:].rearrange("p w t -> p (w t)"),
-            )
-
         acc = {}
+
+        def interleave(copy, g, c0, c1):
+            base = max(b for (gg, b) in x_raw if gg == g and b <= c0)
+            dst = stage.tile([P, c1 - c0, PACK], BF16, name="grouped", bufs=8, align_bytes=64)
+            src = x_raw[(g, base)][:, :, c0 - base : c1 - base].rearrange("p t (c i) -> p c t i", i=RUN)
+            copy(out=dst[:].rearrange("p (c i) t -> p c t i", i=RUN), in_=src)
+            grouped[(g, c0)] = dst
 
         def multiply(j, r, g):
             if g == 0:
@@ -154,108 +156,109 @@ def tile_residual_score_screen_e2_kernel(tc, x, g_words, g_scales, c_prev, inv_s
                 rhs=g_codes[(r, g)].bitcast(E5M2X4),
                 rhs_scale=g_plane[r][:, g, :],
                 start=(g == 0),
-                stop=(g == last),
+                stop=(g == LAST_PASS),
             )
 
-        def z_of(j, r):
-            if r == R_CHUNKS - 1:
-                return z_back[j]
-            return z_front[j // group][:, j % group, r * N : (r + 1) * N]
-
-        for g in range(last):
-            interleave("vector", g, 0, half)
-            interleave("scalar", g, half, D)
-            if g > 0:
-                quantise(g - 1, half, D)
-                for j in range(group, D_TILES):
-                    multiply(j, 0, g - 1)
-            else:
-                nc.vector.tensor_copy(out=inv_col[:], in_=inv_turned[:, 0:D_TILES])
-            quantise(g, 0, half)
-            for j in range(group):
+        def quantise_and_multiply(g, c0, c1):
+            nc.vector.quantize_mx(
+                out=x_codes[g][:, c0:c1].bitcast(E4M3X4),
+                scales=x_plane[g][:, c0:c1],
+                in_=grouped[(g, c0)][:].rearrange("p w t -> p (w t)"),
+            )
+            for j in range(c0 // P, c1 // P):
                 multiply(j, 0, g)
-        quantise(last - 1, half, D)
-        for j in range(group, D_TILES):
-            multiply(j, 0, last - 1)
-        interleave("vector", last, 0, quarter)
-        interleave("scalar", last, quarter, half)
-        interleave("vector", last, half, half + quarter)
-        interleave("scalar", last, half + quarter, D)
-        for u in range(4):
-            quantise(last, u * quarter, (u + 1) * quarter)
-            multiply(2 * u, 0, last)
-            multiply(2 * u + 1, 0, last)
 
-        for j in range(D_TILES):
-            if j % 2 == 0:
-                nc.scalar.activation(out=z_of(j, 0), in_=acc[(j, 0)][:], func=ACT.Copy, scale=inv_col[:, j : j + 1])
+        on_vector = nc.vector.tensor_copy
+        on_scalar = nc.scalar.copy
+        for g in range(LAST_PASS):
+            interleave(on_vector, g, 0, QUARTER)
+            interleave(on_scalar, g, QUARTER, HALF)
+            if g == 0:
+                nc.vector.tensor_copy(out=inv_col[:], in_=inv_turned[:, 0:D_TILES])
+            quantise_and_multiply(g, 0, QUARTER)
+            interleave(on_vector, g, HALF, HALF + QUARTER)
+            interleave(on_scalar, g, HALF + QUARTER, D)
+            quantise_and_multiply(g, QUARTER, HALF)
+            quantise_and_multiply(g, HALF, HALF + QUARTER)
+            if g == LAST_PASS - 1:
+                interleave(on_vector, LAST_PASS, 0, QUARTER)
+            quantise_and_multiply(g, HALF + QUARTER, D)
+        interleave(on_scalar, LAST_PASS, QUARTER, HALF)
+        quantise_and_multiply(LAST_PASS, 0, QUARTER)
+        quantise_and_multiply(LAST_PASS, QUARTER, HALF)
+        for j in range(HALF_TILES, D_TILES):
+            interleave(on_scalar if j % 2 == 0 else on_vector, LAST_PASS, j * P, (j + 1) * P)
+        for j in range(HALF_TILES, D_TILES):
+            quantise_and_multiply(LAST_PASS, j * P, (j + 1) * P)
+
+        def times_inv(out, in_, j, by_scalar):
+            if by_scalar:
+                nc.scalar.activation(out=out, in_=in_, func=ACT.Copy, scale=inv_of(j))
             else:
-                nc.vector.tensor_scalar(
-                    out=z_of(j, 0), in0=acc[(j, 0)][:], scalar1=inv_col[:, j : j + 1], scalar2=None, op0=ALU.mult
-                )
-        for g in range(2):
-            for j in range(D_TILES):
-                multiply(j, 1, g)
+                nc.vector.tensor_scalar(out=out, in0=in_, scalar1=inv_of(j), scalar2=None, op0=ALU.mult)
 
-        def scale_c(j, r):
-            nc.vector.tensor_scalar(
-                out=z_of(j, r), in0=c_raw[(j, r)], scalar1=inv_col[:, j : j + 1], scalar2=None, op0=ALU.mult
-            )
+        def add_times_inv(z, unscaled, j):
+            nc.vector.scalar_tensor_tensor(out=z, in0=unscaled, scalar=inv_of(j), in1=z, op0=ALU.mult, op1=ALU.add)
 
-        def finish(j, z, unscaled):
-            nc.vector.scalar_tensor_tensor(
-                out=z, in0=unscaled, scalar=inv_col[:, j : j + 1], in1=z, op0=ALU.mult, op1=ALU.add
-            )
-
-        def square(src, width, slot):
+        def square(z, width, share):
             squares = stage.tile([P, 2 * N], BF16, name="squares", bufs=2)
             nc.scalar.activation(
-                out=squares[:, 0:width], in_=src, func=ACT.Square, scale=math.sqrt(1.0 / R), accum_out=slot
+                out=squares[:, 0:width], in_=z, func=ACT.Square, scale=math.sqrt(1.0 / R), accum_out=share
             )
 
-        def prepare(j):
-            scale_c(j, 1)
-            finish(j, z_of(j, 0), c_raw[(j, 0)])
+        def store(tile_z, j1, n0, n1):
+            rows = out_0[(j1 - tile_z.shape[1]) * P : j1 * P, n0:n1]
+            nc.sync.dma_start(out=rows.rearrange("(i p) n -> p i n", p=P), in_=tile_z[:])
 
-        ahead = 3
-        for j in range(ahead):
-            prepare(j)
         for j in range(D_TILES):
-            for g in range(2, PASSES):
-                multiply(j, 1, g)
-            finish(j, z_of(j, 1), acc[(j, 1)][:])
-            if j + ahead < D_TILES:
-                prepare(j + ahead)
-            square(z_front[j // group][:, j % group, :], 2 * N, partial[0][:, j : j + 1])
-            if j % group == group - 1:
-                rows = out_0[(j + 1 - group) * P : (j + 1) * P, 0 : 2 * N]
-                nc.sync.dma_start(out=rows.rearrange("(i p) n -> p i n", p=P), in_=z_front[j // group][:])
+            times_inv(z_of(j, 0), acc[(j, 0)][:], j, by_scalar=(j == 0 or j % 2 == 1))
+        for j in range(D_TILES):
+            multiply(j, 1, 0)
 
-        scale_c(0, 2)
+        for j in range(HALF_TILES):
+            times_inv(z_of(j, 1), c_raw[(j, 1)], j, by_scalar=True)
+
+        def add_c_terms(j):
+            if j >= HALF_TILES:
+                times_inv(z_of(j, 1), c_raw[(j, 1)], j, by_scalar=False)
+            add_times_inv(z_of(j, 0), c_raw[(j, 0)], j)
+
+        add_c_terms(0)
+        for j in range(D_TILES):
+            for g in range(1, PASSES):
+                multiply(j, 1, g)
+            add_times_inv(z_of(j, 1), acc[(j, 1)][:], j)
+            if j + 1 < D_TILES:
+                add_c_terms(j + 1)
+            square(z_front[j // HALF_TILES][:, j % HALF_TILES, :], 2 * N, share_front[:, j : j + 1])
+            if j % HALF_TILES == HALF_TILES - 1:
+                store(z_front[j // HALF_TILES], j + 1, 0, 2 * N)
+
+        times_inv(z_back[0], c_raw[(0, LAST_CHUNK)], 0, by_scalar=False)
         for j in range(D_TILES):
             for g in range(PASSES):
-                multiply(j, 2, g)
+                multiply(j, LAST_CHUNK, g)
             if j + 1 < D_TILES:
-                scale_c(j + 1, 2)
-            width = N if j + 1 < D_TILES else 320
-            finish(j, z_back[j][:, 0:width], acc[(j, 2)][:, 0:width])
-            square(z_back[j][:, 0:width], width, partial[1][:, j : j + 1])
+                times_inv(z_back[j + 1], c_raw[(j + 1, LAST_CHUNK)], j + 1, by_scalar=False)
+            width = N if j + 1 < D_TILES else TAIL_SPLIT
+            add_times_inv(z_back[j][:, 0:width], acc[(j, LAST_CHUNK)][:, 0:width], j)
+            square(z_back[j][:, 0:width], width, share_back[:, j : j + 1])
             if width < N:
-                finish(j, z_back[j][:, width:N], acc[(j, 2)][:, width:N])
-                squares_end = keep.tile([P, N - width], F32, name="squares_end")
+                z_tail = z_back[j][:, width:N]
+                add_times_inv(z_tail, acc[(j, LAST_CHUNK)][:, width:N], j)
+                squares_tail = keep.tile([P, N - width], F32, name="squares_tail")
                 nc.vector.scalar_tensor_tensor(
-                    out=squares_end[:], in0=z_back[j][:, width:N], scalar=1.0 / R, in1=z_back[j][:, width:N],
-                    op0=ALU.mult, op1=ALU.mult, accum_out=partial[2][:, j : j + 1],
+                    out=squares_tail[:], in0=z_tail, scalar=1.0 / R, in1=z_tail, op0=ALU.mult, op1=ALU.mult,
+                    accum_out=share_tail[:, j : j + 1],
                 )
-            if j in back_tile:
-                count = back_tile[j].shape[1]
-                rows = out_0[(j + 1 - count) * P : (j + 1) * P, 2 * N : R]
-                nc.sync.dma_start(out=rows.rearrange("(i p) n -> p i n", p=P), in_=back_tile[j][:])
+            if j in back_store:
+                store(back_store[j], j + 1, LAST_CHUNK * N, R)
 
         score_turned = psum.tile([P, P], F32, name="bank0")
-        for s in range(3):
+        for s, share in enumerate(shares):
             nc.tensor.matmul(
-                score_turned[:], lhsT=partial[s][:], rhs=ident_f32[:], is_transpose=True, start=(s == 0), stop=(s == 2)
+                score_turned[:], lhsT=share[:], rhs=ident_f32[:], is_transpose=True, start=(s == 0),
+                stop=(s == len(shares) - 1),
             )
         nc.vector.tensor_copy(out=score_rows[:], in_=score_turned[0:D_TILES, :])
         nc.scalar.dma_start(out=out_1.rearrange("(j p) -> j p", p=P), in_=score_rows[:])

@@ -1,4 +1,3 @@
-import math
 from contextlib import ExitStack
 
 import concourse.mybir as mybir
@@ -12,253 +11,256 @@ BF16 = mybir.dt.bfloat16
 I32 = mybir.dt.int32
 U32 = mybir.dt.uint32
 U8 = mybir.dt.uint8
-E4M3X4 = mybir.dt.float8_e4m3fn_x4
-E5M2X4 = mybir.dt.float8_e5m2_x4
-ACT = mybir.ActivationFunctionType
+E4M3 = mybir.dt.float8_e4m3fn_x4
+E5M2 = mybir.dt.float8_e5m2_x4
 ALU = mybir.AluOpType
+ACT = mybir.ActivationFunctionType
 
 P = 128
 PACK = 4
-K_PASS = P * PACK
-PASSES = T // K_PASS
-BLOCKS = K_PASS // 32
-LAST_PASS = PASSES - 1
-N = 512
-D_TILES = D // P
-HALF_TILES = D_TILES // 2
-R_CHUNKS = R // N
-LAST_CHUNK = R_CHUNKS - 1
-QUADRANT = 32
-SCALE_ROWS = 4
-HALF = D // 2
-QUARTER = D // 4
-RUN = 4
-LAST_CHUNK_STORES = [(0, 4), (4, 6), (6, 7), (7, 8)]
-TAIL_SPLIT = 384
+PASSES = T // (P * PACK)
+NB = 512
+HALF = 512
+ROOT_MEAN = (1.0 / R) ** 0.5
 
 
-def tile_residual_score_screen_e2_kernel(tc, x, g_words, g_scales, c_prev, inv_scale, out_0, out_1):
+def tile_residual_score_screen_e2_kernel(tc, x, g_words, g_scales, c_prev, inv_scale, z_out, score_out):
     nc = tc.nc
-
     with ExitStack() as ctx:
-        keep = ctx.enter_context(tc.tile_pool(name="keep", bufs=1))
-        stage = ctx.enter_context(tc.tile_pool(name="stage", bufs=1))
-        psum = ctx.enter_context(tc.psum_pool(name="psum", bufs=1))
+        sb = ctx.enter_context(tc.tile_pool(name="sb", bufs=1))
+        ps = ctx.enter_context(tc.psum_pool(name="ps", bufs=1))
         ctx.enter_context(tc.manual_schedule())
 
-        g_plane = [keep.tile([P, PASSES, N], U8, name="g_plane%d" % r, align_bytes=64) for r in range(R_CHUNKS)]
-        x_codes = [keep.tile([P, D], U32, name="x_codes%d" % g, align_bytes=64) for g in range(PASSES)]
-        x_plane = [keep.tile([P, D], U8, name="x_plane%d" % g, align_bytes=64) for g in range(PASSES)]
-        ident_bf = keep.tile([P, P], BF16, name="ident_bf")
-        ident_f32 = keep.tile([P, P], F32, name="ident_f32")
-        inv_rows = keep.tile([P, P], BF16, name="inv_rows")
-        inv_col = keep.tile([P, D_TILES], F32, name="inv_col")
-        share_front = keep.tile([P, P], F32, name="share_front")
-        share_back = keep.tile([P, P], F32, name="share_back")
-        share_tail = keep.tile([P, P], F32, name="share_tail")
-        shares = [share_front, share_back, share_tail]
-        score_rows = keep.tile([D_TILES, P], F32, name="score_rows")
-        z_front = [keep.tile([P, HALF_TILES, 2 * N], F32, name="z_front%d" % a) for a in range(2)]
-        z_back = {}
-        back_store = {}
-        for j0, j1 in LAST_CHUNK_STORES:
-            back_store[j1 - 1] = keep.tile([P, j1 - j0, N], F32, name="z_back%d" % j0)
-            for j in range(j0, j1):
-                z_back[j] = back_store[j1 - 1][:, j - j0, :]
+        raw = [[sb.tile([P, PACK, HALF], BF16, name="raw_%d_%d" % (h, g)) for g in range(PASSES)] for h in range(2)]
+        grouped = [sb.tile([P, HALF, PACK], BF16, name="grouped_%d" % g, align_bytes=64) for g in range(PASSES)]
+        x_codes = [[sb.tile([P, HALF], U32, name="xc_%d_%d" % (h, g), align_bytes=64) for g in range(PASSES)] for h in range(2)]
+        x_planes = [[sb.tile([P, HALF], U8, name="xs_%d_%d" % (h, g), align_bytes=64) for g in range(PASSES)] for h in range(2)]
+        g_front = sb.tile([P, PASSES, 2 * NB], U32, name="g_front", align_bytes=64)
+        g_back = sb.tile([P, PASSES, NB], U32, name="g_back", align_bytes=64)
+        plane_first = sb.tile([P, 1, R], U8, name="plane_first", align_bytes=64)
+        plane_rest = sb.tile([P, PASSES - 1, R], U8, name="plane_rest", align_bytes=64)
+        prev = sb.tile([P, 8, R], BF16, name="prev")
+        z = sb.tile([P, 8, R], F32, name="z")
+        inv_rows = sb.tile([P, P], BF16, name="inv_rows")
+        ident_bf = sb.tile([P, P], BF16, name="ident_bf")
+        ident_f = sb.tile([P, P], F32, name="ident_f")
+        inv = sb.tile([P, 8], F32, name="inv")
+        sums = sb.tile([P, 2, P], F32, name="sums")
+        score_rows = sb.tile([P, P], F32, name="score_rows")
+        banks = [ps.tile([P, NB], F32, name="bank_%d" % b) for b in range(8)]
 
-        def z_of(j, r):
-            if r == LAST_CHUNK:
-                return z_back[j]
-            return z_front[j // HALF_TILES][:, j % HALF_TILES, r * N : (r + 1) * N]
+        def cols(n0, n1):
+            return slice(n0 * NB, n1 * NB)
 
-        def inv_of(j):
-            return inv_col[:, j : j + 1]
+        def load_x(h, g):
+            rows = x[g * P * PACK : (g + 1) * P * PACK, h * HALF : (h + 1) * HALF]
+            nc.sync.dma_start(out=raw[h][g][:], in_=rows.rearrange("(p j) w -> p j w", j=PACK))
 
-        words_hbm = g_words.rearrange("g p n t -> p g (n t)")
-        x_raw = {}
-        g_codes = {}
-        c_raw = {}
+        def load_front(g):
+            words = g_words[g].rearrange("p n t -> p (n t)")
+            nc.sync.dma_start(out=g_front[:, g, :].bitcast(I32), in_=words[:, 0 : 2 * NB * PACK].bitcast(I32))
 
-        def load_x(g, c0, c1):
-            raw = keep.tile([P, PACK, c1 - c0], BF16, name="x_raw%d_%d" % (g, c0))
-            rows = x[g * K_PASS : (g + 1) * K_PASS, c0:c1]
-            nc.sync.dma_start(out=raw[:], in_=rows.rearrange("(p t) w -> p t w", t=PACK))
-            x_raw[(g, c0)] = raw
+        def load_back(g0, g1):
+            words = g_words[g0:g1].rearrange("g p n t -> p g (n t)")
+            nc.sync.dma_start(out=g_back[:, g0:g1, :].bitcast(I32), in_=words[:, :, 2 * NB * PACK :].bitcast(I32))
 
-        def load_g(r, g0, g1):
-            words = keep.tile([P, g1 - g0, N], U32, name="g_codes%d_%d" % (r, g0), align_bytes=64)
-            src = words_hbm[:, g0:g1, PACK * N * r : PACK * N * (r + 1)]
-            nc.sync.dma_start(out=words[:].bitcast(I32), in_=src.bitcast(I32))
-            for g in range(g0, g1):
-                g_codes[(r, g)] = words[:, g - g0, :]
+        def load_plane(queue, plane, g0, g1):
+            rows = g_scales[g0:g1].rearrange("g (q r) n -> r q g n", r=4)
+            for r in range(4):
+                queue.dma_start(out=plane[r:P:32].bitcast(I32), in_=rows[r].bitcast(I32))
 
-        def load_scales(r):
-            for s in range(SCALE_ROWS):
-                src = g_scales[:, s:BLOCKS:SCALE_ROWS, N * r : N * (r + 1)].rearrange("g q n -> q g n")
-                nc.sync.dma_start(out=g_plane[r][s:P:QUADRANT, :, :].bitcast(I32), in_=src.bitcast(I32))
+        def load_prev(m0, m1, n0, n1):
+            rows = c_prev[m0 * P : m1 * P, cols(n0, n1)]
+            nc.sync.dma_start(out=prev[:, m0:m1, cols(n0, n1)], in_=rows.rearrange("(m p) n -> p m n", p=P))
 
-        def load_c(j0, j1, r0, r1):
-            raw = keep.tile([P, j1 - j0, (r1 - r0) * N], BF16, name="c_raw%d_%d" % (j0, r0))
-            rows = c_prev[j0 * P : j1 * P, r0 * N : r1 * N]
-            nc.sync.dma_start(out=raw[:], in_=rows.rearrange("(i p) n -> p i n", p=P))
-            for j in range(j0, j1):
-                for r in range(r0, r1):
-                    c_raw[(j, r)] = raw[:, j - j0, (r - r0) * N : (r - r0 + 1) * N]
+        def store_z(m0, m1, n0, n1):
+            rows = z_out[m0 * P : m1 * P, cols(n0, n1)]
+            nc.sync.dma_start(out=rows.rearrange("(m p) n -> p m n", p=P), in_=z[:, m0:m1, cols(n0, n1)])
+
+        def interleave(on_vector, h, g, c0, c1):
+            dst = grouped[g][:, c0:c1, :].rearrange("p (c i) t -> p c t i", i=4)
+            src = raw[h][g][:, :, c0:c1].rearrange("p t (c i) -> p c t i", i=4)
+            if on_vector:
+                nc.vector.tensor_copy(out=dst, in_=src)
+            else:
+                nc.scalar.copy(out=dst, in_=src)
+
+        def quantize(h, g, c0, c1):
+            nc.vector.quantize_mx(
+                out=x_codes[h][g][:, c0:c1].bitcast(E4M3),
+                scales=x_planes[h][g][:, c0:c1],
+                in_=grouped[g][:, c0:c1, :].rearrange("p c t -> p (c t)"),
+            )
+
+        def multiply(b, m, n, g):
+            h, c0 = m // 4, (m % 4) * P
+            words = g_front[:, g, cols(n, n + 1)] if n < 2 else g_back[:, g, :]
+            plane = plane_first[:, 0, cols(n, n + 1)] if g == 0 else plane_rest[:, g - 1, cols(n, n + 1)]
+            nc.tensor.matmul_mx(
+                out=banks[b][:],
+                lhsT=x_codes[h][g][:, c0 : c0 + P].bitcast(E4M3),
+                lhsT_scale=x_planes[h][g][:, c0 : c0 + P],
+                rhs=words.bitcast(E5M2),
+                rhs_scale=plane,
+                start=(g == 0),
+                stop=(g == PASSES - 1),
+            )
+
+        def scale_out(on_vector, b, m, n):
+            if on_vector:
+                nc.vector.tensor_scalar(z[:, m, cols(n, n + 1)], banks[b][:], inv[:, m : m + 1], None, ALU.mult)
+            else:
+                nc.scalar.activation(z[:, m, cols(n, n + 1)], banks[b][:], ACT.Copy, scale=inv[:, m : m + 1])
+
+        def add_prev(m, n0, n1):
+            part = z[:, m, cols(n0, n1)]
+            nc.vector.scalar_tensor_tensor(part, prev[:, m, cols(n0, n1)], inv[:, m : m + 1], part, ALU.mult, ALU.add)
+
+        def scale_prev(on_vector, m, n0, n1):
+            span = cols(n0, n1)
+            if on_vector:
+                nc.vector.tensor_scalar(z[:, m, span], prev[:, m, span], inv[:, m : m + 1], None, ALU.mult)
+            else:
+                nc.scalar.activation(z[:, m, span], prev[:, m, span], ACT.Copy, scale=inv[:, m : m + 1])
+
+        def finish(b, m, n):
+            part = z[:, m, cols(n, n + 1)]
+            nc.vector.scalar_tensor_tensor(part, banks[b][:], inv[:, m : m + 1], part, ALU.mult, ALU.add)
+
+        def square_on_vector(m, n0, n1, slot):
+            part = z[:, m, cols(n0, n1)]
+            nc.vector.scalar_tensor_tensor(
+                prev[:, m, cols(n0, n1)], part, 1.0 / R, part, ALU.mult, ALU.mult, accum_out=sums[:, slot, m : m + 1]
+            )
+
+        def square(m, n0, n1, slot):
+            nc.scalar.activation(
+                prev[:, m, cols(n0, n1)], z[:, m, cols(n0, n1)], ACT.Square, scale=ROOT_MEAN,
+                accum_out=sums[:, slot, m : m + 1],
+            )
 
         nc.vector.memset(inv_rows[:], 0.0)
-        for r in range(R_CHUNKS):
-            nc.vector.memset(g_plane[r][:].rearrange("p g n -> p (g n)").bitcast(I32), 0)
-        for share in shares:
-            nc.vector.memset(share[:], 0.0)
+        nc.vector.memset(plane_first[:].bitcast(I32), 0)
+        nc.vector.memset(plane_rest[:].bitcast(I32), 0)
+        nc.vector.memset(sums[:], 0.0)
         make_identity(nc, ident_bf[:])
-        make_identity(nc, ident_f32[:])
+        make_identity(nc, ident_f[:])
+        load_x(0, 0)
+        nc.scalar.dma_start(out=inv_rows[0:8, :], in_=inv_scale.rearrange("(m p) -> m p", p=P))
+        load_plane(nc.scalar, plane_first, 0, 1)
+        load_plane(nc.gpsimd, plane_rest, 1, PASSES)
+        load_front(0)
+        for g in range(1, PASSES):
+            load_x(0, g)
+            load_front(g)
+        load_back(0, 2)
+        load_prev(0, 2, 0, 2)
+        load_back(2, 3)
+        load_x(1, 0)
+        load_back(3, 5)
+        load_prev(2, 4, 0, 2)
+        load_x(1, 1)
+        load_x(1, 2)
+        load_prev(0, 4, 2, 3)
+        load_x(1, 3)
+        load_x(1, 4)
+        load_prev(4, 6, 0, 3)
+        load_prev(6, 8, 0, 3)
 
-        load_x(0, 0, D)
-        nc.scalar.dma_start(out=inv_rows[0:D_TILES, :], in_=inv_scale.rearrange("(j p) -> j p", p=P))
-        load_scales(0)
-        load_g(0, 0, 1)
-        for g in range(1, LAST_PASS):
-            load_x(g, 0, D)
-            load_g(0, g, g + 1)
-        load_x(LAST_PASS, 0, HALF)
-        load_g(0, LAST_PASS, PASSES)
-        load_x(LAST_PASS, HALF, D)
-        load_scales(1)
-        load_g(1, 0, 1)
-        load_g(1, 1, PASSES)
-        load_c(0, HALF_TILES, 0, LAST_CHUNK)
-        load_c(HALF_TILES, D_TILES, 0, LAST_CHUNK)
-        load_scales(LAST_CHUNK)
-        load_g(LAST_CHUNK, 0, PASSES)
-        load_c(0, D_TILES, LAST_CHUNK, R_CHUNKS)
+        nc.tensor.matmul(banks[7][:, 0:8], lhsT=inv_rows[:], rhs=ident_bf[:, 0:8], start=True, stop=True)
+        nc.scalar.activation(inv[:], banks[7][:, 0:8], ACT.Copy)
 
-        inv_turned = psum.tile([P, P], BF16, name="bank%d" % (D_TILES - 1))
-        nc.tensor.transpose(inv_turned[:], inv_rows[:], ident_bf[:])
+        for g in range(PASSES):
+            interleave(True, 0, g, 0, 256)
+            interleave(False, 0, g, 256, 512)
+            quantize(0, g, 0, 256)
+            quantize(0, g, 256, 512)
+            for b in range(8):
+                multiply(b, b // 2, b % 2, g)
 
-        grouped = {}
-        acc = {}
+        for b in range(4):
+            scale_out(b % 2 == 1, b, b // 2, b % 2)
+        for g in range(3):
+            for m in range(4):
+                multiply(m, m, 2, g)
+        for m in range(4):
+            multiply(m, m, 2, 3)
+            multiply(m, m, 2, 4)
+        for b in range(4, 8):
+            scale_out(False, b, b // 2, b % 2)
+        add_prev(0, 0, 2)
+        add_prev(1, 0, 2)
+        square(0, 0, 2, 0)
+        interleave(True, 1, 0, 0, 512)
+        square(1, 0, 2, 0)
+        add_prev(2, 0, 2)
+        quantize(1, 0, 0, 512)
+        for m in range(4):
+            scale_out(False, m, m, 2)
+        interleave(True, 1, 1, 0, 256)
+        interleave(True, 1, 1, 256, 512)
+        quantize(1, 1, 0, 256)
+        quantize(1, 1, 256, 512)
+        interleave(False, 1, 2, 256, 512)
+        interleave(True, 1, 2, 0, 256)
+        add_prev(3, 0, 2)
+        quantize(1, 2, 0, 512)
+        square(2, 0, 2, 0)
+        interleave(False, 1, 3, 256, 512)
+        interleave(True, 1, 3, 0, 256)
+        interleave(False, 1, 4, 256, 512)
+        interleave(True, 1, 4, 0, 256)
+        quantize(1, 3, 0, 512)
+        add_prev(0, 2, 3)
+        quantize(1, 4, 0, 512)
+        for m in range(1, 4):
+            add_prev(m, 2, 3)
+        scale_prev(False, 4, 0, 2)
+        scale_prev(False, 5, 0, 2)
+        square(0, 2, 3, 1)
+        square(1, 2, 3, 1)
+        scale_prev(False, 6, 0, 2)
+        square(2, 2, 3, 1)
+        square(3, 0, 3, 0)
+        store_z(0, 2, 0, 2)
+        store_z(2, 4, 0, 2)
+        store_z(0, 4, 2, 3)
 
-        def interleave(copy, g, c0, c1):
-            base = max(b for (gg, b) in x_raw if gg == g and b <= c0)
-            dst = stage.tile([P, c1 - c0, PACK], BF16, name="grouped", bufs=8, align_bytes=64)
-            src = x_raw[(g, base)][:, :, c0 - base : c1 - base].rearrange("p t (c i) -> p c t i", i=RUN)
-            copy(out=dst[:].rearrange("p (c i) t -> p c t i", i=RUN), in_=src)
-            grouped[(g, c0)] = dst
+        third = [((4 + i) % 8, 4 + i // 2, i % 2) for i in range(8)]
+        for g in range(3):
+            for b, m, n in third:
+                multiply(b, m, n, g)
+        for b, m, n in third:
+            multiply(b, m, n, 3)
+            multiply(b, m, n, 4)
 
-        def multiply(j, r, g):
-            if g == 0:
-                acc[(j, r)] = psum.tile([P, N], F32, name="bank%d" % j)
-            cols = slice(j * P, (j + 1) * P)
-            nc.tensor.matmul_mx(
-                out=acc[(j, r)][:],
-                lhsT=x_codes[g][:, cols].bitcast(E4M3X4),
-                lhsT_scale=x_plane[g][:, cols],
-                rhs=g_codes[(r, g)].bitcast(E5M2X4),
-                rhs_scale=g_plane[r][:, g, :],
-                start=(g == 0),
-                stop=(g == LAST_PASS),
-            )
+        scale_prev(True, 7, 0, 3)
+        for i in range(4):
+            finish(*third[i])
+        for m in (4, 5):
+            scale_prev(True, m, 2, 3)
+            square(m, 0, 2, 0)
+            store_z(m, m + 1, 0, 2)
+        for i in range(4, 8):
+            finish(*third[i])
+        scale_prev(True, 6, 2, 3)
 
-        def quantise_and_multiply(g, c0, c1):
-            nc.vector.quantize_mx(
-                out=x_codes[g][:, c0:c1].bitcast(E4M3X4),
-                scales=x_plane[g][:, c0:c1],
-                in_=grouped[(g, c0)][:].rearrange("p w t -> p (w t)"),
-            )
-            for j in range(c0 // P, c1 // P):
-                multiply(j, 0, g)
-
-        on_vector = nc.vector.tensor_copy
-        on_scalar = nc.scalar.copy
-        for g in range(LAST_PASS):
-            interleave(on_vector, g, 0, QUARTER)
-            interleave(on_scalar, g, QUARTER, HALF)
-            if g == 0:
-                nc.vector.tensor_copy(out=inv_col[:], in_=inv_turned[:, 0:D_TILES])
-            quantise_and_multiply(g, 0, QUARTER)
-            interleave(on_vector, g, HALF, HALF + QUARTER)
-            interleave(on_scalar, g, HALF + QUARTER, D)
-            quantise_and_multiply(g, QUARTER, HALF)
-            quantise_and_multiply(g, HALF, HALF + QUARTER)
-            if g == LAST_PASS - 1:
-                interleave(on_vector, LAST_PASS, 0, QUARTER)
-            quantise_and_multiply(g, HALF + QUARTER, D)
-        interleave(on_scalar, LAST_PASS, QUARTER, HALF)
-        quantise_and_multiply(LAST_PASS, 0, QUARTER)
-        quantise_and_multiply(LAST_PASS, QUARTER, HALF)
-        for j in range(HALF_TILES, D_TILES):
-            interleave(on_scalar if j % 2 == 0 else on_vector, LAST_PASS, j * P, (j + 1) * P)
-        for j in range(HALF_TILES, D_TILES):
-            quantise_and_multiply(LAST_PASS, j * P, (j + 1) * P)
-
-        def times_inv(out, in_, j, by_scalar):
-            if by_scalar:
-                nc.scalar.activation(out=out, in_=in_, func=ACT.Copy, scale=inv_of(j))
-            else:
-                nc.vector.tensor_scalar(out=out, in0=in_, scalar1=inv_of(j), scalar2=None, op0=ALU.mult)
-
-        def add_times_inv(z, unscaled, j):
-            nc.vector.scalar_tensor_tensor(out=z, in0=unscaled, scalar=inv_of(j), in1=z, op0=ALU.mult, op1=ALU.add)
-
-        def square(z, width, share):
-            squares = stage.tile([P, 2 * N], BF16, name="squares", bufs=2)
-            nc.scalar.activation(
-                out=squares[:, 0:width], in_=z, func=ACT.Square, scale=math.sqrt(1.0 / R), accum_out=share
-            )
-
-        def store(tile_z, j1, n0, n1):
-            rows = out_0[(j1 - tile_z.shape[1]) * P : j1 * P, n0:n1]
-            nc.sync.dma_start(out=rows.rearrange("(i p) n -> p i n", p=P), in_=tile_z[:])
-
-        for j in range(D_TILES):
-            times_inv(z_of(j, 0), acc[(j, 0)][:], j, by_scalar=(j == 0 or j % 2 == 1))
-        for j in range(D_TILES):
-            multiply(j, 1, 0)
-
-        for j in range(HALF_TILES):
-            times_inv(z_of(j, 1), c_raw[(j, 1)], j, by_scalar=True)
-
-        def add_c_terms(j):
-            if j >= HALF_TILES:
-                times_inv(z_of(j, 1), c_raw[(j, 1)], j, by_scalar=False)
-            add_times_inv(z_of(j, 0), c_raw[(j, 0)], j)
-
-        add_c_terms(0)
-        for j in range(D_TILES):
-            for g in range(1, PASSES):
-                multiply(j, 1, g)
-            add_times_inv(z_of(j, 1), acc[(j, 1)][:], j)
-            if j + 1 < D_TILES:
-                add_c_terms(j + 1)
-            square(z_front[j // HALF_TILES][:, j % HALF_TILES, :], 2 * N, share_front[:, j : j + 1])
-            if j % HALF_TILES == HALF_TILES - 1:
-                store(z_front[j // HALF_TILES], j + 1, 0, 2 * N)
-
-        times_inv(z_back[0], c_raw[(0, LAST_CHUNK)], 0, by_scalar=False)
-        for j in range(D_TILES):
+        for m in range(4, 8):
             for g in range(PASSES):
-                multiply(j, LAST_CHUNK, g)
-            if j + 1 < D_TILES:
-                times_inv(z_back[j + 1], c_raw[(j + 1, LAST_CHUNK)], j + 1, by_scalar=False)
-            width = N if j + 1 < D_TILES else TAIL_SPLIT
-            add_times_inv(z_back[j][:, 0:width], acc[(j, LAST_CHUNK)][:, 0:width], j)
-            square(z_back[j][:, 0:width], width, share_back[:, j : j + 1])
-            if width < N:
-                z_tail = z_back[j][:, width:N]
-                add_times_inv(z_tail, acc[(j, LAST_CHUNK)][:, width:N], j)
-                squares_tail = keep.tile([P, N - width], F32, name="squares_tail")
-                nc.vector.scalar_tensor_tensor(
-                    out=squares_tail[:], in0=z_tail, scalar=1.0 / R, in1=z_tail, op0=ALU.mult, op1=ALU.mult,
-                    accum_out=share_tail[:, j : j + 1],
-                )
-            if j in back_store:
-                store(back_store[j], j + 1, LAST_CHUNK * N, R)
+                multiply(m, m, 2, g)
+        for m in (6, 7):
+            square(m, 0, 2, 0)
+            store_z(m, m + 1, 0, 2)
+        for m in range(4, 8):
+            finish(m, m, 2)
+            store_z(m, m + 1, 2, 3)
+            if m == 5:
+                square_on_vector(4, 2, 3, 1)
+        square(5, 2, 3, 1)
+        square(6, 2, 3, 1)
+        square_on_vector(7, 2, 3, 1)
 
-        score_turned = psum.tile([P, P], F32, name="bank0")
-        for s, share in enumerate(shares):
-            nc.tensor.matmul(
-                score_turned[:], lhsT=share[:], rhs=ident_f32[:], is_transpose=True, start=(s == 0),
-                stop=(s == len(shares) - 1),
-            )
-        nc.vector.tensor_copy(out=score_rows[:], in_=score_turned[0:D_TILES, :])
-        nc.scalar.dma_start(out=out_1.rearrange("(j p) -> j p", p=P), in_=score_rows[:])
+        for slot in range(2):
+            nc.tensor.matmul(banks[0][:, 0:P], lhsT=sums[:, slot, :], rhs=ident_f[:], start=(slot == 0), stop=(slot == 1), is_transpose=True)
+        nc.scalar.copy(out=score_rows[:], in_=banks[0][:, 0:P])
+        nc.scalar.dma_start(out=score_out.rearrange("(m p) -> m p", p=P), in_=score_rows[0:8, :])

@@ -139,18 +139,20 @@ def tile_residual_score_screen_e2_kernel(tc, x, g_words, g_scales, c_prev, inv_s
                 accum_out=sums[:, slot, m : m + 1],
             )
 
-        nc.vector.memset(inv_rows[:], 0.0)
         nc.vector.memset(plane_first[:].bitcast(I32), 0)
         nc.vector.memset(plane_rest[:].bitcast(I32), 0)
         nc.vector.memset(sums[:], 0.0)
+        nc.gpsimd.memset(inv_rows[:], 0.0)
         make_identity(nc, ident_bf[:])
         make_identity(nc, ident_f[:])
         load_x(0, 0)
-        nc.scalar.dma_start(out=inv_rows[0:8, :], in_=inv_scale.rearrange("(m p) -> m p", p=P))
-        load_plane(nc.scalar, plane_first, 0, 1)
-        load_plane(nc.gpsimd, plane_rest, 1, PASSES)
+        nc.sync.dma_start(out=inv_rows[0:8, :], in_=inv_scale.rearrange("(m p) -> m p", p=P))
         load_front(0)
-        for g in range(1, PASSES):
+        load_plane(nc.sync, plane_first, 0, 1)
+        load_x(0, 1)
+        load_plane(nc.sync, plane_rest, 1, PASSES)
+        load_front(1)
+        for g in range(2, PASSES):
             load_x(0, g)
             load_front(g)
         load_back(0, 2)

@@ -20,7 +20,7 @@ P = 128
 PACK = 4
 PASSES = T // (P * PACK)
 NB = 512
-HALF = 512
+TILES = D // P
 ROOT_MEAN = (1.0 / R) ** 0.5
 
 
@@ -31,113 +31,93 @@ def tile_residual_score_screen_e2_kernel(tc, x, g_words, g_scales, c_prev, inv_s
         ps = ctx.enter_context(tc.psum_pool(name="ps", bufs=1))
         ctx.enter_context(tc.manual_schedule())
 
-        raw = [[sb.tile([P, PACK, HALF], BF16, name="raw_%d_%d" % (h, g)) for g in range(PASSES)] for h in range(2)]
-        grouped = [sb.tile([P, HALF, PACK], BF16, name="grouped_%d" % g, align_bytes=64) for g in range(PASSES)]
-        x_codes = [[sb.tile([P, HALF], U32, name="xc_%d_%d" % (h, g), align_bytes=64) for g in range(PASSES)] for h in range(2)]
-        x_planes = [[sb.tile([P, HALF], U8, name="xs_%d_%d" % (h, g), align_bytes=64) for g in range(PASSES)] for h in range(2)]
-        g_front = sb.tile([P, PASSES, 2 * NB], U32, name="g_front", align_bytes=64)
-        g_back = sb.tile([P, PASSES, NB], U32, name="g_back", align_bytes=64)
-        plane_first = sb.tile([P, 1, R], U8, name="plane_first", align_bytes=64)
-        plane_rest = sb.tile([P, PASSES - 1, R], U8, name="plane_rest", align_bytes=64)
-        prev = sb.tile([P, 8, R], BF16, name="prev")
-        z = sb.tile([P, 8, R], F32, name="z")
+        raw = [sb.tile([P, PACK, D], BF16, name="raw_%d" % g) for g in range(PASSES)]
+        grouped = [sb.tile([P, D, PACK], BF16, name="grouped_%d" % i, align_bytes=64) for i in range(2)]
+        x_codes = [sb.tile([P, D], U32, name="xc_%d" % g, align_bytes=64) for g in range(PASSES)]
+        x_planes = [sb.tile([P, D], U8, name="xs_%d" % g, align_bytes=64) for g in range(PASSES)]
+        g_first = sb.tile([P, PASSES, NB], U32, name="g_first", align_bytes=64)
+        g_rest = sb.tile([P, PASSES, 2 * NB], U32, name="g_rest", align_bytes=64)
+        plane_first = sb.tile([P, PASSES, NB], U8, name="plane_first", align_bytes=64)
+        plane_rest = sb.tile([P, PASSES, 2 * NB], U8, name="plane_rest", align_bytes=64)
+        prev = sb.tile([P, TILES, R], BF16, name="prev")
+        z = sb.tile([P, TILES, R], F32, name="z")
         inv_rows = sb.tile([P, P], BF16, name="inv_rows")
         ident_bf = sb.tile([P, P], BF16, name="ident_bf")
         ident_f = sb.tile([P, P], F32, name="ident_f")
-        inv = sb.tile([P, 8], F32, name="inv")
-        sums = sb.tile([P, 2, P], F32, name="sums")
+        inv = sb.tile([P, TILES], F32, name="inv")
+        sums = sb.tile([P, 4, P], F32, name="sums")
         score_rows = sb.tile([P, P], F32, name="score_rows")
         banks = [ps.tile([P, NB], F32, name="bank_%d" % b) for b in range(8)]
 
         def cols(n0, n1):
             return slice(n0 * NB, n1 * NB)
 
-        def load_x(h, g):
-            rows = x[g * P * PACK : (g + 1) * P * PACK, h * HALF : (h + 1) * HALF]
-            nc.sync.dma_start(out=raw[h][g][:], in_=rows.rearrange("(p j) w -> p j w", j=PACK))
+        def load_x(g):
+            rows = x[g * P * PACK : (g + 1) * P * PACK, :]
+            nc.sync.dma_start(out=raw[g][:], in_=rows.rearrange("(p j) w -> p j w", j=PACK))
 
-        def load_front(g):
-            words = g_words[g].rearrange("p n t -> p (n t)")
-            nc.sync.dma_start(out=g_front[:, g, :].bitcast(I32), in_=words[:, 0 : 2 * NB * PACK].bitcast(I32))
+        def load_words(tile, g0, g1, n0, n1):
+            words = g_words[g0:g1].rearrange("g p n t -> p g (n t)")[:, :, n0 * NB * PACK : n1 * NB * PACK]
+            nc.sync.dma_start(out=tile[:, g0:g1, :].bitcast(I32), in_=words.bitcast(I32))
 
-        def load_back(g0, g1):
-            words = g_words[g0:g1].rearrange("g p n t -> p g (n t)")
-            nc.sync.dma_start(out=g_back[:, g0:g1, :].bitcast(I32), in_=words[:, :, 2 * NB * PACK :].bitcast(I32))
-
-        def load_plane(queue, plane, g0, g1):
-            rows = g_scales[g0:g1].rearrange("g (q r) n -> r q g n", r=4)
+        def load_plane(plane, n0, n1):
+            rows = g_scales[:, :, cols(n0, n1)].rearrange("g (q r) n -> r q g n", r=4)
             for r in range(4):
-                queue.dma_start(out=plane[r:P:32].bitcast(I32), in_=rows[r].bitcast(I32))
+                nc.sync.dma_start(out=plane[r:P:32].bitcast(I32), in_=rows[r].bitcast(I32))
 
-        def load_prev(m0, m1, n0, n1):
-            rows = c_prev[m0 * P : m1 * P, cols(n0, n1)]
-            nc.sync.dma_start(out=prev[:, m0:m1, cols(n0, n1)], in_=rows.rearrange("(m p) n -> p m n", p=P))
+        def load_prev(m0, m1):
+            rows = c_prev[m0 * P : m1 * P, :]
+            nc.sync.dma_start(out=prev[:, m0:m1, :], in_=rows.rearrange("(m p) n -> p m n", p=P))
 
-        def store_z(m0, m1, n0, n1):
-            rows = z_out[m0 * P : m1 * P, cols(n0, n1)]
-            nc.sync.dma_start(out=rows.rearrange("(m p) n -> p m n", p=P), in_=z[:, m0:m1, cols(n0, n1)])
+        def store_z(m, n0, n1):
+            nc.sync.dma_start(out=z_out[m * P : (m + 1) * P, cols(n0, n1)], in_=z[:, m, cols(n0, n1)])
 
-        def interleave(on_vector, h, g, c0, c1):
-            dst = grouped[g][:, c0:c1, :].rearrange("p (c i) t -> p c t i", i=4)
-            src = raw[h][g][:, :, c0:c1].rearrange("p t (c i) -> p c t i", i=4)
+        def interleave(on_vector, g, m0, m1):
+            dst = grouped[g % 2][:, m0 * P : m1 * P, :]
+            src = raw[g][:, :, m0 * P : m1 * P].rearrange("p t c -> p c t")
             if on_vector:
                 nc.vector.tensor_copy(out=dst, in_=src)
             else:
                 nc.scalar.copy(out=dst, in_=src)
 
-        def quantize(h, g, c0, c1):
+        def quantize(g, m0, m1):
+            span = slice(m0 * P, m1 * P)
             nc.vector.quantize_mx(
-                out=x_codes[h][g][:, c0:c1].bitcast(E4M3),
-                scales=x_planes[h][g][:, c0:c1],
-                in_=grouped[g][:, c0:c1, :].rearrange("p c t -> p (c t)"),
+                out=x_codes[g][:, span].bitcast(E4M3),
+                scales=x_planes[g][:, span],
+                in_=grouped[g % 2][:, span, :].rearrange("p c t -> p (c t)"),
             )
 
         def multiply(b, m, n, g):
-            h, c0 = m // 4, (m % 4) * P
-            words = g_front[:, g, cols(n, n + 1)] if n < 2 else g_back[:, g, :]
-            plane = plane_first[:, 0, cols(n, n + 1)] if g == 0 else plane_rest[:, g - 1, cols(n, n + 1)]
+            words = g_first[:, g, :] if n == 0 else g_rest[:, g, cols(n - 1, n)]
+            plane = plane_first[:, g, :] if n == 0 else plane_rest[:, g, cols(n - 1, n)]
             nc.tensor.matmul_mx(
                 out=banks[b][:],
-                lhsT=x_codes[h][g][:, c0 : c0 + P].bitcast(E4M3),
-                lhsT_scale=x_planes[h][g][:, c0 : c0 + P],
+                lhsT=x_codes[g][:, m * P : (m + 1) * P].bitcast(E4M3),
+                lhsT_scale=x_planes[g][:, m * P : (m + 1) * P],
                 rhs=words.bitcast(E5M2),
                 rhs_scale=plane,
                 start=(g == 0),
                 stop=(g == PASSES - 1),
             )
 
-        def scale_out(on_vector, b, m, n):
+        def scale_into_z(on_vector, source, m, n0, n1):
             if on_vector:
-                nc.vector.tensor_scalar(z[:, m, cols(n, n + 1)], banks[b][:], inv[:, m : m + 1], None, ALU.mult)
+                nc.vector.tensor_scalar(z[:, m, cols(n0, n1)], source, inv[:, m : m + 1], None, ALU.mult)
             else:
-                nc.scalar.activation(z[:, m, cols(n, n + 1)], banks[b][:], ACT.Copy, scale=inv[:, m : m + 1])
+                nc.scalar.activation(z[:, m, cols(n0, n1)], source, ACT.Copy, scale=inv[:, m : m + 1])
 
-        def add_prev(m, n0, n1):
-            part = z[:, m, cols(n0, n1)]
-            nc.vector.scalar_tensor_tensor(part, prev[:, m, cols(n0, n1)], inv[:, m : m + 1], part, ALU.mult, ALU.add)
+        def scale_and_add(source, m, span):
+            part = z[:, m, span]
+            nc.vector.scalar_tensor_tensor(part, source, inv[:, m : m + 1], part, ALU.mult, ALU.add)
 
-        def scale_prev(on_vector, m, n0, n1):
-            span = cols(n0, n1)
+        def square(on_vector, m, span, slot):
+            part = z[:, m, span]
+            total = sums[:, slot, m : m + 1]
             if on_vector:
-                nc.vector.tensor_scalar(z[:, m, span], prev[:, m, span], inv[:, m : m + 1], None, ALU.mult)
+                nc.vector.scalar_tensor_tensor(prev[:, m, span], part, 1.0 / R, part, ALU.mult, ALU.mult, accum_out=total)
             else:
-                nc.scalar.activation(z[:, m, span], prev[:, m, span], ACT.Copy, scale=inv[:, m : m + 1])
-
-        def finish(b, m, n):
-            part = z[:, m, cols(n, n + 1)]
-            nc.vector.scalar_tensor_tensor(part, banks[b][:], inv[:, m : m + 1], part, ALU.mult, ALU.add)
-
-        def square_on_vector(m, n0, n1, slot):
-            part = z[:, m, cols(n0, n1)]
-            nc.vector.scalar_tensor_tensor(
-                prev[:, m, cols(n0, n1)], part, 1.0 / R, part, ALU.mult, ALU.mult, accum_out=sums[:, slot, m : m + 1]
-            )
-
-        def square(m, n0, n1, slot):
-            nc.scalar.activation(
-                prev[:, m, cols(n0, n1)], z[:, m, cols(n0, n1)], ACT.Square, scale=ROOT_MEAN,
-                accum_out=sums[:, slot, m : m + 1],
-            )
+                nc.scalar.activation(prev[:, m, span], part, ACT.Square, scale=ROOT_MEAN, accum_out=total)
 
         nc.vector.memset(plane_first[:].bitcast(I32), 0)
         nc.vector.memset(plane_rest[:].bitcast(I32), 0)
@@ -145,124 +125,107 @@ def tile_residual_score_screen_e2_kernel(tc, x, g_words, g_scales, c_prev, inv_s
         nc.gpsimd.memset(inv_rows[:], 0.0)
         make_identity(nc, ident_bf[:])
         make_identity(nc, ident_f[:])
-        load_x(0, 0)
-        nc.sync.dma_start(out=inv_rows[0:8, :], in_=inv_scale.rearrange("(m p) -> m p", p=P))
-        load_front(0)
-        load_plane(nc.sync, plane_first, 0, 1)
-        load_x(0, 1)
-        load_plane(nc.sync, plane_rest, 1, PASSES)
-        load_front(1)
-        for g in range(2, PASSES):
-            load_x(0, g)
-            load_front(g)
-        load_back(0, 2)
-        load_prev(0, 2, 0, 2)
-        load_back(2, 3)
-        load_x(1, 0)
-        load_back(3, 5)
-        load_prev(2, 4, 0, 2)
-        load_x(1, 1)
-        load_x(1, 2)
-        load_prev(0, 4, 2, 3)
-        load_x(1, 3)
-        load_x(1, 4)
-        load_prev(4, 6, 0, 3)
-        load_prev(6, 8, 0, 3)
+        load_x(0)
+        nc.sync.dma_start(out=inv_rows[0:TILES, :], in_=inv_scale.rearrange("(m p) -> m p", p=P))
+        load_words(g_first, 0, 1, 0, 1)
+        load_plane(plane_first, 0, 1)
+        for g in range(1, PASSES):
+            load_x(g)
+            load_words(g_first, g, g + 1, 0, 1)
+        load_plane(plane_rest, 1, 3)
+        load_words(g_rest, 0, 1, 1, 3)
+        load_words(g_rest, 1, 2, 1, 3)
+        load_prev(0, 2)
+        load_words(g_rest, 2, 3, 1, 3)
+        load_words(g_rest, 3, 4, 1, 3)
+        load_prev(2, 4)
+        load_words(g_rest, 4, 5, 1, 3)
+        load_prev(4, 6)
+        load_prev(6, 8)
 
-        nc.tensor.matmul(banks[7][:, 0:8], lhsT=inv_rows[:], rhs=ident_bf[:, 0:8], start=True, stop=True)
-        nc.scalar.activation(inv[:], banks[7][:, 0:8], ACT.Copy)
+        nc.tensor.matmul(banks[7][:, 0:TILES], lhsT=inv_rows[:], rhs=ident_bf[:, 0:TILES], start=True, stop=True)
+        nc.scalar.activation(inv[:], banks[7][:, 0:TILES], ACT.Copy)
 
-        for g in range(PASSES):
-            interleave(True, 0, g, 0, 256)
-            interleave(False, 0, g, 256, 512)
-            quantize(0, g, 0, 256)
-            quantize(0, g, 256, 512)
+        for g in range(PASSES - 1):
+            interleave(True, g, 0, 2)
+            interleave(False, g, 4, 6)
+            interleave(True, g, 2, 4)
+            interleave(False, g, 6, 8)
+            for m in range(0, TILES, 2):
+                quantize(g, m, m + 2)
+            for m in range(TILES):
+                multiply(m, m, 0, g)
+        g = PASSES - 1
+        interleave(True, g, 0, 1)
+        interleave(False, g, 2, 4)
+        interleave(True, g, 1, 2)
+        quantize(g, 0, 1)
+        interleave(True, g, 4, 5)
+        quantize(g, 1, 2)
+        interleave(False, g, 6, 7)
+        interleave(True, g, 5, 6)
+        quantize(g, 2, 4)
+        interleave(True, g, 7, 8)
+        quantize(g, 4, 6)
+        quantize(g, 6, 8)
+        for m in range(TILES):
+            multiply(m, m, 0, g)
+        for m in range(TILES):
+            scale_into_z(m in (3, 5, 7), banks[m][:], m, 0, 1)
+
+        for g in range(3):
             for b in range(8):
-                multiply(b, b // 2, b % 2, g)
-
-        for b in range(4):
-            scale_out(b % 2 == 1, b, b // 2, b % 2)
-        for g in range(3):
-            for m in range(4):
-                multiply(m, m, 2, g)
-        for m in range(4):
-            multiply(m, m, 2, 3)
-            multiply(m, m, 2, 4)
+                multiply(b, b // 2, 1 + b % 2, g)
+        for g in (3, 4):
+            for b in range(4):
+                multiply(b, b // 2, 1 + b % 2, g)
         for b in range(4, 8):
-            scale_out(False, b, b // 2, b % 2)
-        add_prev(0, 0, 2)
-        add_prev(1, 0, 2)
-        square(0, 0, 2, 0)
-        interleave(True, 1, 0, 0, 512)
-        square(1, 0, 2, 0)
-        add_prev(2, 0, 2)
-        quantize(1, 0, 0, 512)
+            for g in (3, 4):
+                multiply(b, b // 2, 1 + b % 2, g)
+
+        def start_rows(on_vector, m):
+            scale_and_add(prev[:, m, cols(0, 1)], m, cols(0, 1))
+            scale_into_z(on_vector, prev[:, m, cols(1, 3)], m, 1, 3)
+
+        def finish_rows(m):
+            for n in (1, 2):
+                scale_and_add(banks[2 * (m % 4) + n - 1][:], m, cols(n, n + 1))
+
         for m in range(4):
-            scale_out(False, m, m, 2)
-        interleave(True, 1, 1, 0, 256)
-        interleave(True, 1, 1, 256, 512)
-        quantize(1, 1, 0, 256)
-        quantize(1, 1, 256, 512)
-        interleave(False, 1, 2, 256, 512)
-        interleave(True, 1, 2, 0, 256)
-        add_prev(3, 0, 2)
-        quantize(1, 2, 0, 512)
-        square(2, 0, 2, 0)
-        interleave(False, 1, 3, 256, 512)
-        interleave(True, 1, 3, 0, 256)
-        interleave(False, 1, 4, 256, 512)
-        interleave(True, 1, 4, 0, 256)
-        quantize(1, 3, 0, 512)
-        add_prev(0, 2, 3)
-        quantize(1, 4, 0, 512)
-        for m in range(1, 4):
-            add_prev(m, 2, 3)
-        scale_prev(False, 4, 0, 2)
-        scale_prev(False, 5, 0, 2)
-        square(0, 2, 3, 1)
-        square(1, 2, 3, 1)
-        scale_prev(False, 6, 0, 2)
-        square(2, 2, 3, 1)
-        square(3, 0, 3, 0)
-        store_z(0, 2, 0, 2)
-        store_z(2, 4, 0, 2)
-        store_z(0, 4, 2, 3)
+            start_rows(True, m)
+        for m in range(4):
+            finish_rows(m)
+            store_z(m, 0, 3)
+        start_rows(False, 4)
+        square(False, 0, cols(0, 3), 0)
+        start_rows(False, 5)
+        square(False, 1, cols(0, 3), 0)
 
-        third = [((4 + i) % 8, 4 + i // 2, i % 2) for i in range(8)]
-        for g in range(3):
-            for b, m, n in third:
-                multiply(b, m, n, g)
-        for b, m, n in third:
-            multiply(b, m, n, 3)
-            multiply(b, m, n, 4)
-
-        scale_prev(True, 7, 0, 3)
-        for i in range(4):
-            finish(*third[i])
-        for m in (4, 5):
-            scale_prev(True, m, 2, 3)
-            square(m, 0, 2, 0)
-            store_z(m, m + 1, 0, 2)
-        for i in range(4, 8):
-            finish(*third[i])
-        scale_prev(True, 6, 2, 3)
-
-        for m in range(4, 8):
+        for b in range(8):
             for g in range(PASSES):
-                multiply(m, m, 2, g)
-        for m in (6, 7):
-            square(m, 0, 2, 0)
-            store_z(m, m + 1, 0, 2)
-        for m in range(4, 8):
-            finish(m, m, 2)
-            store_z(m, m + 1, 2, 3)
-            if m == 5:
-                square_on_vector(4, 2, 3, 1)
-        square(5, 2, 3, 1)
-        square(6, 2, 3, 1)
-        square_on_vector(7, 2, 3, 1)
+                multiply(b, 4 + b // 2, 1 + b % 2, g)
+        finish_rows(4)
+        start_rows(True, 6)
+        start_rows(True, 7)
+        square(False, 2, cols(0, 3), 0)
+        square(False, 3, cols(0, 3), 0)
+        for m in range(4, 7):
+            if m > 4:
+                finish_rows(m)
+            store_z(m, 0, 3)
+            square(False, m, cols(0, 3), 0)
+        scale_and_add(banks[6][:], 7, cols(1, 2))
+        store_z(7, 0, 2)
+        square(True, 7, cols(0, 1), 0)
+        square(False, 7, cols(1, 2), 1)
+        halves = [slice(2 * NB + i * NB // 2, 2 * NB + (i + 1) * NB // 2) for i in range(2)]
+        for i in range(2):
+            scale_and_add(banks[7][:, i * NB // 2 : (i + 1) * NB // 2], 7, halves[i])
+        store_z(7, 2, 3)
+        square(True, 7, halves[0], 2)
+        square(False, 7, halves[1], 3)
 
-        for slot in range(2):
-            nc.tensor.matmul(banks[0][:, 0:P], lhsT=sums[:, slot, :], rhs=ident_f[:], start=(slot == 0), stop=(slot == 1), is_transpose=True)
+        for slot in range(4):
+            nc.tensor.matmul(banks[0][:, 0:P], lhsT=sums[:, slot, :], rhs=ident_f[:], start=(slot == 0), stop=(slot == 3), is_transpose=True)
         nc.scalar.copy(out=score_rows[:], in_=banks[0][:, 0:P])
-        nc.scalar.dma_start(out=score_out.rearrange("(m p) -> m p", p=P), in_=score_rows[0:8, :])
+        nc.scalar.dma_start(out=score_out.rearrange("(m p) -> m p", p=P), in_=score_rows[0:TILES, :])

@@ -38,7 +38,8 @@ def tile_residual_score_screen_e2_kernel(tc, x, g_words, g_scales, c_prev, inv_s
         g_first = sb.tile([P, PASSES, NB], U32, name="g_first", align_bytes=64)
         g_rest = sb.tile([P, PASSES, 2 * NB], U32, name="g_rest", align_bytes=64)
         plane_first = sb.tile([P, PASSES, NB], U8, name="plane_first", align_bytes=64)
-        plane_rest = sb.tile([P, PASSES, 2 * NB], U8, name="plane_rest", align_bytes=64)
+        plane_early = sb.tile([P, 2, 2 * NB], U8, name="plane_early", align_bytes=64)
+        plane_late = sb.tile([P, PASSES - 2, 2 * NB], U8, name="plane_late", align_bytes=64)
         prev = sb.tile([P, TILES, R], BF16, name="prev")
         z = sb.tile([P, TILES, R], F32, name="z")
         inv_rows = sb.tile([P, P], BF16, name="inv_rows")
@@ -60,8 +61,8 @@ def tile_residual_score_screen_e2_kernel(tc, x, g_words, g_scales, c_prev, inv_s
             words = g_words[g0:g1].rearrange("g p n t -> p g (n t)")[:, :, n0 * NB * PACK : n1 * NB * PACK]
             nc.sync.dma_start(out=tile[:, g0:g1, :].bitcast(I32), in_=words.bitcast(I32))
 
-        def load_plane(plane, n0, n1):
-            rows = g_scales[:, :, cols(n0, n1)].rearrange("g (q r) n -> r q g n", r=4)
+        def load_plane(plane, g0, g1, n0, n1):
+            rows = g_scales[g0:g1, :, cols(n0, n1)].rearrange("g (q r) n -> r q g n", r=4)
             for r in range(4):
                 nc.sync.dma_start(out=plane[r:P:32].bitcast(I32), in_=rows[r].bitcast(I32))
 
@@ -73,8 +74,8 @@ def tile_residual_score_screen_e2_kernel(tc, x, g_words, g_scales, c_prev, inv_s
             nc.sync.dma_start(out=z_out[m * P : (m + 1) * P, cols(n0, n1)], in_=z[:, m, cols(n0, n1)])
 
         def interleave(on_vector, g, m0, m1):
-            dst = grouped[g % 2][:, m0 * P : m1 * P, :]
-            src = raw[g][:, :, m0 * P : m1 * P].rearrange("p t c -> p c t")
+            dst = grouped[g % 2][:, m0 * P : m1 * P, :].rearrange("p (c i) t -> p c t i", i=4)
+            src = raw[g][:, :, m0 * P : m1 * P].rearrange("p t (c i) -> p c t i", i=4)
             if on_vector:
                 nc.vector.tensor_copy(out=dst, in_=src)
             else:
@@ -90,7 +91,12 @@ def tile_residual_score_screen_e2_kernel(tc, x, g_words, g_scales, c_prev, inv_s
 
         def multiply(b, m, n, g):
             words = g_first[:, g, :] if n == 0 else g_rest[:, g, cols(n - 1, n)]
-            plane = plane_first[:, g, :] if n == 0 else plane_rest[:, g, cols(n - 1, n)]
+            if n == 0:
+                plane = plane_first[:, g, :]
+            elif g < 2:
+                plane = plane_early[:, g, cols(n - 1, n)]
+            else:
+                plane = plane_late[:, g - 2, cols(n - 1, n)]
             nc.tensor.matmul_mx(
                 out=banks[b][:],
                 lhsT=x_codes[g][:, m * P : (m + 1) * P].bitcast(E4M3),
@@ -119,24 +125,28 @@ def tile_residual_score_screen_e2_kernel(tc, x, g_words, g_scales, c_prev, inv_s
             else:
                 nc.scalar.activation(prev[:, m, span], part, ACT.Square, scale=ROOT_MEAN, accum_out=total)
 
+        nc.vector.memset(inv_rows[:], 0.0)
         nc.vector.memset(plane_first[:].bitcast(I32), 0)
-        nc.vector.memset(plane_rest[:].bitcast(I32), 0)
+        nc.vector.memset(ident_bf[:], 0.0)
+        nc.vector.memset(ident_f[:], 0.0)
+        nc.vector.memset(plane_early[:].bitcast(I32), 0)
+        nc.vector.memset(plane_late[:].bitcast(I32), 0)
         nc.vector.memset(sums[:], 0.0)
-        nc.gpsimd.memset(inv_rows[:], 0.0)
-        make_identity(nc, ident_bf[:])
-        make_identity(nc, ident_f[:])
+        make_identity(nc, ident_bf[:], nomemset=True)
+        make_identity(nc, ident_f[:], nomemset=True)
         load_x(0)
         nc.sync.dma_start(out=inv_rows[0:TILES, :], in_=inv_scale.rearrange("(m p) -> m p", p=P))
         load_words(g_first, 0, 1, 0, 1)
-        load_plane(plane_first, 0, 1)
+        load_plane(plane_first, 0, PASSES, 0, 1)
         for g in range(1, PASSES):
             load_x(g)
             load_words(g_first, g, g + 1, 0, 1)
-        load_plane(plane_rest, 1, 3)
+        load_plane(plane_early, 0, 2, 1, 3)
         load_words(g_rest, 0, 1, 1, 3)
         load_words(g_rest, 1, 2, 1, 3)
-        load_prev(0, 2)
+        load_plane(plane_late, 2, PASSES, 1, 3)
         load_words(g_rest, 2, 3, 1, 3)
+        load_prev(0, 2)
         load_words(g_rest, 3, 4, 1, 3)
         load_prev(2, 4)
         load_words(g_rest, 4, 5, 1, 3)
@@ -146,77 +156,68 @@ def tile_residual_score_screen_e2_kernel(tc, x, g_words, g_scales, c_prev, inv_s
         nc.tensor.matmul(banks[7][:, 0:TILES], lhsT=inv_rows[:], rhs=ident_bf[:, 0:TILES], start=True, stop=True)
         nc.scalar.activation(inv[:], banks[7][:, 0:TILES], ACT.Copy)
 
-        for g in range(PASSES - 1):
-            interleave(True, g, 0, 2)
-            interleave(False, g, 4, 6)
-            interleave(True, g, 2, 4)
-            interleave(False, g, 6, 8)
+        for g in range(PASSES):
+            for m in range(1, TILES, 2):
+                interleave(False, g, m, m + 1)
+            interleave(True, g, 0, 1)
             for m in range(0, TILES, 2):
-                quantize(g, m, m + 2)
+                if m + 2 < TILES:
+                    interleave(True, g, m + 2, m + 3)
+                quantize(g, m, m + 1)
+                quantize(g, m + 1, m + 2)
             for m in range(TILES):
                 multiply(m, m, 0, g)
-        g = PASSES - 1
-        interleave(True, g, 0, 1)
-        interleave(False, g, 2, 4)
-        interleave(True, g, 1, 2)
-        quantize(g, 0, 1)
-        interleave(True, g, 4, 5)
-        quantize(g, 1, 2)
-        interleave(False, g, 6, 7)
-        interleave(True, g, 5, 6)
-        quantize(g, 2, 4)
-        interleave(True, g, 7, 8)
-        quantize(g, 4, 6)
-        quantize(g, 6, 8)
         for m in range(TILES):
-            multiply(m, m, 0, g)
-        for m in range(TILES):
-            scale_into_z(m in (3, 5, 7), banks[m][:], m, 0, 1)
+            scale_into_z(m % 2 == 1, banks[m][:], m, 0, 1)
 
-        for g in range(3):
+        for g in range(PASSES):
             for b in range(8):
                 multiply(b, b // 2, 1 + b % 2, g)
-        for g in (3, 4):
-            for b in range(4):
-                multiply(b, b // 2, 1 + b % 2, g)
-        for b in range(4, 8):
-            for g in (3, 4):
-                multiply(b, b // 2, 1 + b % 2, g)
 
-        def start_rows(on_vector, m):
+        def add_prev(m):
             scale_and_add(prev[:, m, cols(0, 1)], m, cols(0, 1))
+
+        def scale_prev(on_vector, m):
             scale_into_z(on_vector, prev[:, m, cols(1, 3)], m, 1, 3)
 
-        def finish_rows(m):
-            for n in (1, 2):
-                scale_and_add(banks[2 * (m % 4) + n - 1][:], m, cols(n, n + 1))
+        def finish(m, n):
+            scale_and_add(banks[2 * (m % 4) + n - 1][:], m, cols(n, n + 1))
 
         for m in range(4):
-            start_rows(True, m)
+            add_prev(m)
+            scale_prev(True, m)
+            square(False, m, cols(0, 1), 0)
+        scale_prev(False, 4)
         for m in range(4):
-            finish_rows(m)
+            finish(m, 1)
+            finish(m, 2)
             store_z(m, 0, 3)
-        start_rows(False, 4)
-        square(False, 0, cols(0, 3), 0)
-        start_rows(False, 5)
-        square(False, 1, cols(0, 3), 0)
+            square(False, m, cols(1, 3), 1)
+            if m == 0:
+                scale_prev(False, 5)
 
         for b in range(8):
             for g in range(PASSES):
                 multiply(b, 4 + b // 2, 1 + b % 2, g)
-        finish_rows(4)
-        start_rows(True, 6)
-        start_rows(True, 7)
-        square(False, 2, cols(0, 3), 0)
-        square(False, 3, cols(0, 3), 0)
-        for m in range(4, 7):
-            if m > 4:
-                finish_rows(m)
+        for m in (4, 5):
+            add_prev(m)
+            finish(m, 1)
+            if m == 5:
+                scale_prev(True, 6)
+            finish(m, 2)
             store_z(m, 0, 3)
             square(False, m, cols(0, 3), 0)
-        scale_and_add(banks[6][:], 7, cols(1, 2))
-        store_z(7, 0, 2)
+        add_prev(6)
+        finish(6, 1)
+        scale_prev(True, 7)
+        add_prev(7)
+        square(False, 6, cols(0, 2), 0)
+        finish(6, 2)
+        store_z(6, 0, 3)
         square(True, 7, cols(0, 1), 0)
+        square(False, 6, cols(2, 3), 1)
+        finish(7, 1)
+        store_z(7, 0, 2)
         square(False, 7, cols(1, 2), 1)
         halves = [slice(2 * NB + i * NB // 2, 2 * NB + (i + 1) * NB // 2) for i in range(2)]
         for i in range(2):

from contextlib import ExitStack

import concourse.mybir as mybir
from concourse.masks import make_identity

T, D, R = 2560, 1024, 1536
FLOPS = 2 * T * D * R

F32 = mybir.dt.float32
BF16 = mybir.dt.bfloat16
I32 = mybir.dt.int32
U32 = mybir.dt.uint32
U8 = mybir.dt.uint8
E4M3 = mybir.dt.float8_e4m3fn_x4
E5M2 = mybir.dt.float8_e5m2_x4
ALU = mybir.AluOpType
ACT = mybir.ActivationFunctionType

P = 128
PACK = 4
PASSES = T // (P * PACK)
NB = 512
TILES = D // P
ROOT_MEAN = (1.0 / R) ** 0.5


def tile_residual_score_screen_e2_kernel(tc, x, g_words, g_scales, c_prev, inv_scale, z_out, score_out):
    nc = tc.nc
    with ExitStack() as ctx:
        sb = ctx.enter_context(tc.tile_pool(name="sb", bufs=1))
        ps = ctx.enter_context(tc.psum_pool(name="ps", bufs=1))
        ctx.enter_context(tc.manual_schedule())

        raw = [sb.tile([P, PACK, D], BF16, name="raw_%d" % g) for g in range(PASSES)]
        grouped = [sb.tile([P, D, PACK], BF16, name="grouped_%d" % i, align_bytes=64) for i in range(2)]
        x_codes = [sb.tile([P, D], U32, name="xc_%d" % g, align_bytes=64) for g in range(PASSES)]
        x_planes = [sb.tile([P, D], U8, name="xs_%d" % g, align_bytes=64) for g in range(PASSES)]
        g_first = sb.tile([P, PASSES, NB], U32, name="g_first", align_bytes=64)
        g_rest = sb.tile([P, PASSES, 2 * NB], U32, name="g_rest", align_bytes=64)
        plane_first = sb.tile([P, PASSES, NB], U8, name="plane_first", align_bytes=64)
        plane_early = sb.tile([P, 2, 2 * NB], U8, name="plane_early", align_bytes=64)
        plane_late = sb.tile([P, PASSES - 2, 2 * NB], U8, name="plane_late", align_bytes=64)
        prev = sb.tile([P, TILES, R], BF16, name="prev")
        z = sb.tile([P, TILES, R], F32, name="z")
        inv_rows = sb.tile([P, P], BF16, name="inv_rows")
        ident_bf = sb.tile([P, P], BF16, name="ident_bf")
        ident_f = sb.tile([P, P], F32, name="ident_f")
        inv = sb.tile([P, TILES], F32, name="inv")
        sums = sb.tile([P, 4, P], F32, name="sums")
        score_rows = sb.tile([P, P], F32, name="score_rows")
        banks = [ps.tile([P, NB], F32, name="bank_%d" % b) for b in range(8)]

        def cols(n0, n1):
            return slice(n0 * NB, n1 * NB)

        def load_x(g):
            rows = x[g * P * PACK : (g + 1) * P * PACK, :]
            nc.sync.dma_start(out=raw[g][:], in_=rows.rearrange("(p j) w -> p j w", j=PACK))

        def load_words(tile, g0, g1, n0, n1):
            words = g_words[g0:g1].rearrange("g p n t -> p g (n t)")[:, :, n0 * NB * PACK : n1 * NB * PACK]
            nc.sync.dma_start(out=tile[:, g0:g1, :].bitcast(I32), in_=words.bitcast(I32))

        def load_plane(plane, g0, g1, n0, n1):
            rows = g_scales[g0:g1, :, cols(n0, n1)].rearrange("g (q r) n -> r q g n", r=4)
            for r in range(4):
                nc.sync.dma_start(out=plane[r:P:32].bitcast(I32), in_=rows[r].bitcast(I32))

        def load_prev(m0, m1):
            rows = c_prev[m0 * P : m1 * P, :]
            nc.sync.dma_start(out=prev[:, m0:m1, :], in_=rows.rearrange("(m p) n -> p m n", p=P))

        def store_z(m, n0, n1):
            nc.sync.dma_start(out=z_out[m * P : (m + 1) * P, cols(n0, n1)], in_=z[:, m, cols(n0, n1)])

        def interleave(on_vector, g, m0, m1):
            dst = grouped[g % 2][:, m0 * P : m1 * P, :].rearrange("p (c i) t -> p c t i", i=4)
            src = raw[g][:, :, m0 * P : m1 * P].rearrange("p t (c i) -> p c t i", i=4)
            if on_vector:
                nc.vector.tensor_copy(out=dst, in_=src)
            else:
                nc.scalar.copy(out=dst, in_=src)

        def quantize(g, m0, m1):
            span = slice(m0 * P, m1 * P)
            nc.vector.quantize_mx(
                out=x_codes[g][:, span].bitcast(E4M3),
                scales=x_planes[g][:, span],
                in_=grouped[g % 2][:, span, :].rearrange("p c t -> p (c t)"),
            )

        def multiply(b, m, n, g):
            words = g_first[:, g, :] if n == 0 else g_rest[:, g, cols(n - 1, n)]
            if n == 0:
                plane = plane_first[:, g, :]
            elif g < 2:
                plane = plane_early[:, g, cols(n - 1, n)]
            else:
                plane = plane_late[:, g - 2, cols(n - 1, n)]
            nc.tensor.matmul_mx(
                out=banks[b][:],
                lhsT=x_codes[g][:, m * P : (m + 1) * P].bitcast(E4M3),
                lhsT_scale=x_planes[g][:, m * P : (m + 1) * P],
                rhs=words.bitcast(E5M2),
                rhs_scale=plane,
                start=(g == 0),
                stop=(g == PASSES - 1),
            )

        def scale_into_z(on_vector, source, m, n0, n1):
            if on_vector:
                nc.vector.tensor_scalar(z[:, m, cols(n0, n1)], source, inv[:, m : m + 1], None, ALU.mult)
            else:
                nc.scalar.activation(z[:, m, cols(n0, n1)], source, ACT.Copy, scale=inv[:, m : m + 1])

        def scale_and_add(source, m, span):
            part = z[:, m, span]
            nc.vector.scalar_tensor_tensor(part, source, inv[:, m : m + 1], part, ALU.mult, ALU.add)

        def square(on_vector, m, span, slot):
            part = z[:, m, span]
            total = sums[:, slot, m : m + 1]
            if on_vector:
                nc.vector.scalar_tensor_tensor(prev[:, m, span], part, 1.0 / R, part, ALU.mult, ALU.mult, accum_out=total)
            else:
                nc.scalar.activation(prev[:, m, span], part, ACT.Square, scale=ROOT_MEAN, accum_out=total)

        nc.vector.memset(inv_rows[:], 0.0)
        nc.vector.memset(plane_first[:].bitcast(I32), 0)
        nc.vector.memset(ident_bf[:], 0.0)
        nc.vector.memset(ident_f[:], 0.0)
        nc.vector.memset(plane_early[:].bitcast(I32), 0)
        nc.vector.memset(plane_late[:].bitcast(I32), 0)
        nc.vector.memset(sums[:], 0.0)
        make_identity(nc, ident_bf[:], nomemset=True)
        make_identity(nc, ident_f[:], nomemset=True)
        load_x(0)
        nc.sync.dma_start(out=inv_rows[0:TILES, :], in_=inv_scale.rearrange("(m p) -> m p", p=P))
        load_words(g_first, 0, 1, 0, 1)
        load_plane(plane_first, 0, PASSES, 0, 1)
        for g in range(1, PASSES):
            load_x(g)
            load_words(g_first, g, g + 1, 0, 1)
        load_plane(plane_early, 0, 2, 1, 3)
        load_words(g_rest, 0, 1, 1, 3)
        load_words(g_rest, 1, 2, 1, 3)
        load_plane(plane_late, 2, PASSES, 1, 3)
        load_words(g_rest, 2, 3, 1, 3)
        load_prev(0, 2)
        load_words(g_rest, 3, 4, 1, 3)
        load_prev(2, 4)
        load_words(g_rest, 4, 5, 1, 3)
        load_prev(4, 6)
        load_prev(6, 8)

        nc.tensor.matmul(banks[7][:, 0:TILES], lhsT=inv_rows[:], rhs=ident_bf[:, 0:TILES], start=True, stop=True)
        nc.scalar.activation(inv[:], banks[7][:, 0:TILES], ACT.Copy)

        for g in range(PASSES):
            for m in range(1, TILES, 2):
                interleave(False, g, m, m + 1)
            interleave(True, g, 0, 1)
            for m in range(0, TILES, 2):
                if m + 2 < TILES:
                    interleave(True, g, m + 2, m + 3)
                quantize(g, m, m + 1)
                quantize(g, m + 1, m + 2)
            for m in range(TILES):
                multiply(m, m, 0, g)
        for m in range(TILES):
            scale_into_z(m % 2 == 1, banks[m][:], m, 0, 1)

        for g in range(PASSES):
            for b in range(8):
                multiply(b, b // 2, 1 + b % 2, g)

        def add_prev(m):
            scale_and_add(prev[:, m, cols(0, 1)], m, cols(0, 1))

        def scale_prev(on_vector, m):
            scale_into_z(on_vector, prev[:, m, cols(1, 3)], m, 1, 3)

        def finish(m, n):
            scale_and_add(banks[2 * (m % 4) + n - 1][:], m, cols(n, n + 1))

        for m in range(4):
            add_prev(m)
            scale_prev(True, m)
            square(False, m, cols(0, 1), 0)
        scale_prev(False, 4)
        for m in range(4):
            finish(m, 1)
            finish(m, 2)
            store_z(m, 0, 3)
            square(False, m, cols(1, 3), 1)
            if m == 0:
                scale_prev(False, 5)

        for b in range(8):
            for g in range(PASSES):
                multiply(b, 4 + b // 2, 1 + b % 2, g)
        for m in (4, 5):
            add_prev(m)
            finish(m, 1)
            if m == 5:
                scale_prev(True, 6)
            finish(m, 2)
            store_z(m, 0, 3)
            square(False, m, cols(0, 3), 0)
        add_prev(6)
        finish(6, 1)
        scale_prev(True, 7)
        add_prev(7)
        square(False, 6, cols(0, 2), 0)
        finish(6, 2)
        store_z(6, 0, 3)
        square(True, 7, cols(0, 1), 0)
        square(False, 6, cols(2, 3), 1)
        finish(7, 1)
        store_z(7, 0, 2)
        square(False, 7, cols(1, 2), 1)
        halves = [slice(2 * NB + i * NB // 2, 2 * NB + (i + 1) * NB // 2) for i in range(2)]
        for i in range(2):
            scale_and_add(banks[7][:, i * NB // 2 : (i + 1) * NB // 2], 7, halves[i])
        store_z(7, 2, 3)
        square(True, 7, halves[0], 2)
        square(False, 7, halves[1], 3)

        for slot in range(4):
            nc.tensor.matmul(banks[0][:, 0:P], lhsT=sums[:, slot, :], rhs=ident_f[:], start=(slot == 0), stop=(slot == 3), is_transpose=True)
        nc.scalar.copy(out=score_rows[:], in_=banks[0][:, 0:P])
        nc.scalar.dma_start(out=score_out.rearrange("(m p) -> m p", p=P), in_=score_rows[0:TILES, :])
